import numpy as np
import ml_dtypes


def mxq(x, axis, fmt="e4m3"):
    dtype, down = {"e4m3": (ml_dtypes.float8_e4m3fn, 7), "e5m2": (ml_dtypes.float8_e5m2, 14)}[fmt]
    v = np.moveaxis(np.asarray(x, np.float32).astype(ml_dtypes.bfloat16).astype(np.float64), axis, -1)
    blocks = v.reshape(v.shape[:-1] + (-1, 32))
    amax = np.abs(blocks).max(-1, keepdims=True)
    byte = np.maximum(np.where(amax > 0, np.frexp(amax)[1] - 1 + 127, 0) - down, 1)
    scale = np.exp2(byte - 127.0)
    codes = (blocks / scale).astype(np.float32).astype(dtype).astype(np.float64)
    return np.moveaxis((codes * scale).reshape(v.shape), -1, axis)


WIDE = False


def mx_kscale(k):
    if not WIDE:
        return np.ones(k)
    levels = np.array([10, -10, 5, -5, 0])
    if k % 512:
        return np.exp2(np.random.permutation(np.resize(levels, k // 32))).repeat(32)
    a = np.empty((k // 512, 16))
    for p in range(k // 512):
        a[p, :8] = np.random.permutation(np.resize(levels, 8))
        for g in range(8):
            far = levels[np.abs(levels - a[p, g]) >= 10]
            a[p, g + 8] = far[np.random.randint(len(far))]
    return np.exp2(a.ravel()).repeat(32)


def f64(x):
    return np.asarray(x).astype(np.float64)


def striped(idx):
    return np.tile(idx.reshape(-1, 16).T, (8, 1)).astype(np.uint16)


def unstriped(offs):
    return offs[:16].T.reshape(-1).astype(np.int64)


E2M1 = np.array([0.0, 0.5, 1.0, 1.5, 2.0, 3.0, 4.0, 6.0, -0.0, -0.5, -1.0, -1.5, -2.0, -3.0, -4.0, -6.0])


def pack_weight(w, fmt):
    k, n = w.shape
    w = f64(np.asarray(w, np.float32).astype(ml_dtypes.bfloat16)).reshape(k // 32, 32, n)
    amax = np.abs(w).max(1)
    if fmt == "e4m3":
        byte = np.frexp(amax)[1] - 1 + 127 - 7
    else:
        mant, ex = np.frexp(amax / 6.0)
        byte = np.where(mant > 0.5, ex, ex - 1) + 127
    byte = np.clip(np.where(amax > 0, byte, 1), 1, 254)
    scaled = (w * np.exp2(127.0 - byte)[:, None, :]).reshape(k, n).astype(np.float32)
    by_word = np.ascontiguousarray(scaled.reshape(k // 512, 128, 4, n).transpose(0, 1, 3, 2))
    if fmt == "e4m3":
        words = by_word.astype(ml_dtypes.float8_e4m3fn).view(np.uint8)
    else:
        c = by_word.astype(ml_dtypes.float4_e2m1fn).view(np.uint8) & 0xF
        words = (c[..., 0::2] | (c[..., 1::2] << 4)).reshape(k // 512, 128, 2 * n)
    return np.ascontiguousarray(words), np.ascontiguousarray(byte.astype(np.uint8).reshape(k // 512, 16, n))


def unpack_weight(words, scales, fmt):
    g, _, n = scales.shape
    words = np.ascontiguousarray(words).reshape(g, 128, n, -1)
    if fmt == "e4m3":
        vals = words.view(ml_dtypes.float8_e4m3fn).astype(np.float64)
    else:
        nib = np.empty((g, 128, n, 4), np.uint8)
        nib[..., 0::2] = words & 0xF
        nib[..., 1::2] = words >> 4
        vals = E2M1[nib]
    vals = vals * np.repeat(np.exp2(scales.astype(np.float64) - 127.0), 8, axis=1)[..., None]
    return vals.transpose(0, 1, 3, 2).reshape(g * 512, n)


def gelu(v):
    return 0.5 * v * (1.0 + np.tanh(np.sqrt(2.0 / np.pi) * (v + 0.044715 * v**3)))


def bf(x):
    return np.asarray(x, np.float32).astype(ml_dtypes.bfloat16)

def planes(Y):
    n, m = Y.shape
    b = f64(bf(Y)).reshape(n // 32, 32, m)
    amax = np.abs(b).max(1)
    byte = np.clip(np.where(amax > 0, np.frexp(amax)[1] - 1 + 127 - 7, 1), 1, 254)
    codes = (b * np.exp2(127.0 - byte)[:, None, :]).reshape(n, m).astype(np.float32).astype(ml_dtypes.float8_e4m3fn).view(np.uint8)
    words = codes.reshape(n // 512, 128, 4, m).transpose(0, 1, 3, 2)
    return np.ascontiguousarray(words), np.ascontiguousarray(byte.astype(np.uint8).reshape(n // 512, 16, m))


K, T, S, H, N = 1024, 4096, 1024, 512, 512

def setup_inputs():
    n = np.random.standard_normal
    s = mx_kscale(K)[:, None]
    u = mx_kscale(H)[:, None]
    size = np.exp(0.8 * n(N))
    tab_words, tab_scales = pack_weight(n((K, T)) * s, "e4m3")
    wa_words, wa_scales = pack_weight(n((K, H)) / np.sqrt(K) / s * u.T, "e2m1")
    wb_words, wb_scales = pack_weight(n((K, H)) / np.sqrt(K) / s * u.T, "e4m3")
    wc = n((K, H)) / np.sqrt(K) / s * u.T
    wf = 1.5 * n((H, N)) / np.sqrt(H) / u * size[None, :]
    return {
        "tab_words": tab_words, "tab_scales": tab_scales,
        "offs": striped(np.random.permutation(T)[:S]),
        "offs2": striped(np.random.permutation(T)[:S]),
        "offs3": striped(np.random.permutation(T)[:S]),
        "wa_words": wa_words, "wa_scales": wa_scales,
        "wb_words": wb_words, "wb_scales": wb_scales,
        "wc": wc.astype(np.float32), "wf": wf.astype(np.float32),
        "bf": (0.5 * n(N) * size).astype(np.float32),
    }

def reference(tab_words, tab_scales, offs, offs2, offs3, wa_words, wa_scales, wb_words, wb_scales, wc, wf, bf):
    va = unpack_weight(tab_words, tab_scales, "e4m3")[:, unstriped(offs)]
    vb = unpack_weight(tab_words, tab_scales, "e4m3")[:, unstriped(offs2)]
    vc = unpack_weight(tab_words, tab_scales, "e4m3")[:, unstriped(offs3)]
    a = unpack_weight(wa_words, wa_scales, "e2m1").T @ va
    b = unpack_weight(wb_words, wb_scales, "e4m3").T @ vb
    c = mxq(f64(wc), 0, "e4m3").T @ vc
    h = np.maximum(np.minimum(a, b), np.minimum(np.maximum(a, b), c))
    y = (mxq(f64(wf), 0, "e4m3").T @ mxq(h, 0, "e4m3")) + f64(bf)[:, None]
    words, scales = planes(y)
    return y, words, scales

@@ -1,0 +1,281 @@
+from contextlib import ExitStack
+
+import concourse.mybir as mybir
+
+K, T, S, H, N = 1024, 4096, 1024, 512, 512
+FLOPS = 2 * (3 * K * H * S + H * N * S)
+
+F32 = mybir.dt.float32
+BF16 = mybir.dt.bfloat16
+I32 = mybir.dt.int32
+U32 = mybir.dt.uint32
+U16 = mybir.dt.uint16
+U8 = mybir.dt.uint8
+FP8X4 = mybir.dt.float8_e4m3fn_x4
+FP4X4 = mybir.dt.float4_e2m1fn_x4
+MIN = mybir.AluOpType.min
+MAX = mybir.AluOpType.max
+IDENTITY = mybir.ActivationFunctionType.Identity
+
+P = 128
+PACK = 4
+PASSES = K // (P * PACK)
+HALF = S // 2
+BLOCK = 128
+CHUNKS = ((0, 256), (256, 256), (512, 256), (768, 128), (896, 128))
+QUADS = 4
+
+
+def tile_list_triplex_median_fault_kernel(
+    tc, tab_words, tab_scales, offs, offs2, offs3, wa_words, wa_scales, wb_words, wb_scales, wc, wf, bf,
+    out_0, out_1, out_2,
+):
+    nc = tc.nc
+    with ExitStack() as ctx:
+        keep = ctx.enter_context(tc.tile_pool(name="keep", bufs=1))
+        picked = ctx.enter_context(tc.tile_pool(name="picked", bufs=8))
+        stage = ctx.enter_context(tc.tile_pool(name="stage", bufs=PASSES))
+        work = ctx.enter_context(tc.tile_pool(name="work", bufs=3))
+        psum = ctx.enter_context(tc.psum_pool(name="psum", bufs=1))
+
+        def kept(name, width, dtype):
+            return keep.tile([P, width], dtype, name=name, align_bytes=64)
+
+        lists = [keep.tile([P, S // 16], U16, name=f"list{x}") for x in range(3)]
+        scale_win = kept("scale_win", T, U8)
+        word_win = [kept("word_win0", T, I32)]
+        wc_raw = [stage.tile([P, PACK * H], F32, name="raw", align_bytes=64) for a in range(PASSES)]
+        wa_raw = kept("wa_raw", PASSES * 2 * H, U8)
+        ws_raw = kept("ws_raw", 2 * H, U8)
+        ws_rows = keep.tile([P, 2 * H], U8, name="ws_rows", tag="late_words", align_bytes=64)
+        w_scales = kept("w_scales", PASSES * 2 * H, U8)
+        bias = kept("bias", PACK, F32)
+        picked_rows = keep.tile([P, 3 * S], U8, name="picked_rows", tag="late_wb", align_bytes=64)
+        picked_scales = kept("picked_scales", PASSES * 3 * S, U8)
+
+        nc.vector.memset(scale_win[:].bitcast(I32), 0)
+        nc.vector.memset(ws_raw[:].bitcast(I32), 0)
+        nc.vector.memset(w_scales[:].bitcast(I32), 0)
+        nc.vector.memset(picked_scales[:].bitcast(I32), 0)
+        warm = kept("warm", 16, F32)
+        nc.vector.memset(warm[:, 0:1], 0.0)
+        nc.scalar.activation(warm[:, 8:9], warm[:, 0:1], IDENTITY)
+
+        def load_scale_rows(dst, src):
+            nc.sync.dma_start(dst[0:P:4, :].bitcast(I32), src.rearrange("a q t -> q a t").bitcast(I32))
+
+        def place_scale_rows(dst, src):
+            for q in range(QUADS):
+                nc.scalar.dma_start(
+                    dst[32 * q : 32 * q + 4, :].bitcast(I32).rearrange("r (a w) -> r a w", a=PASSES),
+                    src[32 * q : 32 * q + 32 : 4, :].bitcast(I32),
+                )
+
+        def load_words(a):
+            nc.sync.dma_start(word_win[a][:], tab_words[a].rearrange("p t i -> p (t i)").bitcast(I32))
+
+        def deal(dst, src, run):
+            nc.vector.tensor_copy(
+                dst.rearrange("p (a t q w) -> p a t q w", a=2, t=PACK, w=run),
+                src.rearrange("p (a q t w) -> p a t q w", a=2, t=PACK, w=run),
+            )
+
+        nc.sync.dma_start(lists[0][:], offs)
+        load_scale_rows(scale_win[:], tab_scales)
+        load_scale_rows(ws_raw[:, 0:H], wa_scales)
+        load_scale_rows(ws_raw[:, H : 2 * H], wb_scales)
+        nc.sync.dma_start(lists[1][:], offs2)
+        nc.sync.dma_start(lists[2][:], offs3)
+        load_words(0)
+        for a in range(PASSES):
+            nc.sync.dma_start(wc_raw[a][:], wc[512 * a : 512 * (a + 1), :].rearrange("(p j) r -> p (j r)", j=PACK))
+        nc.sync.dma_start(
+            wa_raw[:].bitcast(I32).rearrange("p (a w) -> p a w", a=PASSES),
+            wa_words.bitcast(I32).rearrange("a p w -> p a w"),
+        )
+        nc.sync.dma_start(bias[:], bf.rearrange("(p t) -> p t", t=PACK))
+
+        deal(ws_rows[:].bitcast(I32), ws_raw[:].bitcast(I32), 2)
+        place_scale_rows(w_scales[:], ws_rows[:])
+        word_win.append(keep.tile([P, T], I32, name="word_win1", tag="late_words", align_bytes=64))
+        load_words(1)
+
+        for x in range(3):
+            nc.vector.tensor_copy(picked_rows[:, x * S : (x + 1) * S], scale_win[:].indirect(lists[x][:]))
+        place_scale_rows(picked_scales[:], picked_rows[:])
+        wb_raw = keep.tile([P, PASSES * H], I32, name="wb_raw", tag="late_wb", align_bytes=64)
+        nc.sync.dma_start(
+            wb_raw[:].rearrange("p (a w) -> p a w", a=PASSES),
+            wb_words.rearrange("a p e i -> a p (e i)").bitcast(I32).rearrange("a p w -> p a w"),
+        )
+
+        words = {}
+
+        def gather(x, a, half):
+            g = picked.tile([P, HALF], U32, name="g", align_bytes=64)
+            cols = slice(half * HALF // 16, (half + 1) * HALF // 16)
+            nc.vector.tensor_copy(g[:], word_win[a][:].bitcast(U32).indirect(lists[x][:, cols]))
+            words[x, a, half] = g
+
+        wa_codes = kept("wa_codes", PASSES * 2 * H, U8)
+        wb_codes = kept("wb_codes", PASSES * H, I32)
+        wc_codes = [kept(f"wc_codes{a}", H, U32) for a in range(PASSES)]
+        wc_scales = [kept(f"wc_scales{a}", H, U8) for a in range(PASSES)]
+
+        def stationary(x, a, t):
+            lo = a * H + t * P
+            s0 = (2 * a + x) * H + t * P
+            if x == 0:
+                return wa_codes[:, 2 * lo : 2 * (lo + P)].bitcast(FP4X4), w_scales[:, s0 : s0 + P]
+            if x == 1:
+                return wb_codes[:, lo : lo + P].bitcast(FP8X4), w_scales[:, s0 : s0 + P]
+            return wc_codes[a][:, t * P : (t + 1) * P].bitcast(FP8X4), wc_scales[a][:, t * P : (t + 1) * P]
+
+        sums = [[kept(f"sum{x}_{half}", PACK * HALF, BF16) for half in range(2)] for x in range(3)]
+
+        def project(x, half):
+            for blk in range(HALF // BLOCK):
+                bank = psum.tile([P, PACK, BLOCK], F32, name=f"bank{half * (HALF // BLOCK) + blk}")
+                j0 = blk * BLOCK
+                for t in range(PACK):
+                    for a in range(PASSES):
+                        codes, scales = stationary(x, a, t)
+                        s0 = (a * 3 + x) * S + half * HALF + j0
+                        nc.tensor.matmul_mx(
+                            out=bank[:, t, :], lhsT=codes, lhsT_scale=scales,
+                            rhs=words[x, a, half][:, j0 : j0 + BLOCK].bitcast(FP8X4),
+                            rhs_scale=picked_scales[:, s0 : s0 + BLOCK],
+                            start=(a == 0), stop=(a == PASSES - 1),
+                        )
+                nc.scalar.copy(
+                    sums[x][half][:, PACK * j0 : PACK * (j0 + BLOCK)].rearrange("p (j t) -> p j t", t=PACK),
+                    bank[:].rearrange("p t j -> p j t"),
+                )
+
+        for x in range(2):
+            for half in range(2):
+                gather(x, 0, half)
+
+        wc_bf = [kept(f"wc_bf{a}", PACK * H, BF16) for a in range(PASSES)]
+        for a in range(PASSES):
+            dst = wc_bf[a][:].rearrange("p (t q u i j) -> p u q t j i", t=PACK, u=2, i=4, j=PACK)
+            src = wc_raw[a][:].rearrange("p (j q t u i) -> p u q t j i", t=PACK, u=2, i=4, j=PACK)
+            for u in range(2):
+                nc.scalar.copy(dst[:, u], src[:, u])
+        wf_raw = stage.tile([P, PACK * N], F32, name="raw", align_bytes=64)
+        wf_rows = wf.rearrange("(q t i) n -> t q i n", t=PACK, i=8)
+        for t in range(PACK):
+            nc.sync.dma_start(wf_raw[:, t * N : (t + 1) * N], wf_rows[t])
+        deal(wa_codes[:].bitcast(I32), wa_raw[:].bitcast(I32), 4)
+        for half in range(2):
+            gather(0, 1, half)
+            project(0, half)
+        deal(wb_codes[:], wb_raw[:], 8)
+        for half in range(2):
+            gather(1, 1, half)
+            project(1, half)
+        for a in range(PASSES):
+            nc.vector.quantize_mx(out=wc_codes[a][:].bitcast(FP8X4), scales=wc_scales[a][:], in_=wc_bf[a][:])
+        for half in range(2):
+            for a in range(PASSES):
+                gather(2, a, half)
+            project(2, half)
+
+        wf_bf = kept("wf_bf", PACK * N, BF16)
+        nc.scalar.copy(
+            wf_bf[:].rearrange("p (t m j) -> p m j t", t=PACK, j=PACK),
+            wf_raw[:].rearrange("p (j m t) -> p m j t", t=PACK, j=PACK),
+        )
+        wf_codes = kept("wf_codes", N, U32)
+        wf_scales = kept("wf_scales", N, U8)
+        nc.vector.quantize_mx(out=wf_codes[:].bitcast(FP8X4), scales=wf_scales[:], in_=wf_bf[:])
+
+        y_scales = kept("y_scales", S, U8)
+        y_rows = out_0.rearrange("(p t) j -> p t j", t=PACK)
+        y_words = out_1[0].rearrange("p m i -> p (m i)").bitcast(I32)
+        last = len(CHUNKS) - 1
+        state = {}
+
+        def part(x, c):
+            j0, width = CHUNKS[c]
+            half, off = divmod(j0, HALF)
+            return sums[x][half][:, PACK * off : PACK * (off + width)]
+
+        def pick(name, c, in0, in1, op):
+            out = work.tile([P, PACK * CHUNKS[c][1]], BF16, name=name, align_bytes=64)
+            nc.vector.tensor_tensor(out[:], in0, in1, op)
+            state[name, c] = out[:]
+
+        def high(c):
+            pick("high", c, part(0, c), part(1, c), MAX)
+
+        def low(c):
+            pick("low", c, part(0, c), part(1, c), MIN)
+
+        def clip(c):
+            pick("clip", c, state["high", c], part(2, c), MIN)
+
+        def median(c):
+            pick("median", c, state["low", c], state["clip", c], MAX)
+
+        def score(c):
+            j0, width = CHUNKS[c]
+            h_codes = work.tile([P, width], U32, name="h_codes", align_bytes=64)
+            h_scales = work.tile([P, width], U8, name="h_scales", align_bytes=64)
+            nc.vector.quantize_mx(out=h_codes[:].bitcast(FP8X4), scales=h_scales[:], in_=state["median", c])
+            y = kept(f"y{c}", PACK * width, F32)
+            for pair in range(2):
+                bank = psum.tile([P, 2, width], F32, name=f"bank{7 - pair}")
+                for u in range(2):
+                    t = 2 * pair + u
+                    nc.tensor.matmul_mx(
+                        out=bank[:, u, :], lhsT=wf_codes[:, t * P : (t + 1) * P].bitcast(FP8X4),
+                        lhsT_scale=wf_scales[:, t * P : (t + 1) * P],
+                        rhs=h_codes[:].bitcast(FP8X4), rhs_scale=h_scales[:], start=True, stop=True,
+                    )
+                for u in range(2):
+                    t = 2 * pair + u
+                    nc.scalar.activation(
+                        y[:, t * width : (t + 1) * width], bank[:, u, :], IDENTITY, bias=bias[:, t : t + 1]
+                    )
+            nc.sync.dma_start(y_rows[:, :, j0 : j0 + width], y[:].rearrange("p (t j) -> p t j", t=PACK))
+            state["y", c] = y
+
+        def weave(c):
+            y_bf = kept(f"y_bf{c}", PACK * CHUNKS[c][1], BF16)
+            copy = nc.vector.tensor_copy if c >= last - 1 else nc.scalar.copy
+            copy(
+                y_bf[:].rearrange("p (c i t) -> p c t i", t=PACK, i=4),
+                state["y", c][:].rearrange("p (t c i) -> p c t i", t=PACK, i=4),
+            )
+            state["y_bf", c] = y_bf
+
+        def planes(c):
+            j0, width = CHUNKS[c]
+            y_codes = kept(f"y_codes{c}", width, U32)
+            nc.vector.quantize_mx(
+                out=y_codes[:].bitcast(FP8X4), scales=y_scales[:, j0 : j0 + width], in_=state["y_bf", c][:]
+            )
+            nc.sync.dma_start(y_words[:, j0 : j0 + width], y_codes[:].bitcast(I32))
+
+        high(0)
+        low(0)
+        for c in range(len(CHUNKS)):
+            clip(c)
+            if c < last:
+                high(c + 1)
+            median(c)
+            if c < last:
+                low(c + 1)
+            if c >= 2:
+                planes(c - 2)
+            score(c)
+            if c < last - 1:
+                weave(c)
+        weave(last - 1)
+        weave(last)
+        planes(last - 1)
+        planes(last)
+        for q in range(QUADS):
+            eng = nc.scalar if q % 2 else nc.sync
+            eng.dma_start(out_2[0, 4 * q : 4 * q + 4, :].bitcast(I32), y_scales[32 * q : 32 * q + 4, :].bitcast(I32))

@@ -22,8 +22,12 @@ PACK = 4
 PASSES = K // (P * PACK)
 HALF = S // 2
 BLOCK = 128
-CHUNKS = ((0, 256), (256, 256), (512, 256), (768, 128), (896, 128))
+BANKS = HALF // BLOCK
+CHUNK = 256
+CHUNKS = S // CHUNK
 QUADS = 4
+ROWS = 32
+SCALAR_WEAVES = ()
 
 
 def tile_list_triplex_median_fault_kernel(
@@ -33,46 +37,40 @@ def tile_list_triplex_median_fault_kernel(
     nc = tc.nc
     with ExitStack() as ctx:
         keep = ctx.enter_context(tc.tile_pool(name="keep", bufs=1))
-        picked = ctx.enter_context(tc.tile_pool(name="picked", bufs=8))
-        stage = ctx.enter_context(tc.tile_pool(name="stage", bufs=PASSES))
-        work = ctx.enter_context(tc.tile_pool(name="work", bufs=3))
+        work = ctx.enter_context(tc.tile_pool(name="work", bufs=2))
         psum = ctx.enter_context(tc.psum_pool(name="psum", bufs=1))
 
-        def kept(name, width, dtype):
-            return keep.tile([P, width], dtype, name=name, align_bytes=64)
+        def kept(name, width, dtype, tag=None):
+            return keep.tile([P, width], dtype, name=name, tag=tag or name, align_bytes=64)
 
         lists = [keep.tile([P, S // 16], U16, name=f"list{x}") for x in range(3)]
         scale_win = kept("scale_win", T, U8)
         word_win = [kept("word_win0", T, I32)]
-        wc_raw = [stage.tile([P, PACK * H], F32, name="raw", align_bytes=64) for a in range(PASSES)]
         wa_raw = kept("wa_raw", PASSES * 2 * H, U8)
         ws_raw = kept("ws_raw", 2 * H, U8)
-        ws_rows = keep.tile([P, 2 * H], U8, name="ws_rows", tag="late_words", align_bytes=64)
+        ws_rows = kept("ws_rows", 2 * H, U8, tag="late_words")
         w_scales = kept("w_scales", PASSES * 2 * H, U8)
         bias = kept("bias", PACK, F32)
-        picked_rows = keep.tile([P, 3 * S], U8, name="picked_rows", tag="late_wb", align_bytes=64)
+        picked_rows = kept("picked_rows", 3 * S, U8, tag="late_wb")
         picked_scales = kept("picked_scales", PASSES * 3 * S, U8)
 
-        nc.vector.memset(scale_win[:].bitcast(I32), 0)
-        nc.vector.memset(ws_raw[:].bitcast(I32), 0)
-        nc.vector.memset(w_scales[:].bitcast(I32), 0)
-        nc.vector.memset(picked_scales[:].bitcast(I32), 0)
-        warm = kept("warm", 16, F32)
-        nc.vector.memset(warm[:, 0:1], 0.0)
-        nc.scalar.activation(warm[:, 8:9], warm[:, 0:1], IDENTITY)
-
-        def load_scale_rows(dst, src):
-            nc.sync.dma_start(dst[0:P:4, :].bitcast(I32), src.rearrange("a q t -> q a t").bitcast(I32))
+        def load_scale_rows(eng, dst, src):
+            eng.dma_start(dst[0:ROWS, :].bitcast(I32), src.rearrange("a q t -> q a t").bitcast(I32))
 
         def place_scale_rows(dst, src):
             for q in range(QUADS):
                 nc.scalar.dma_start(
                     dst[32 * q : 32 * q + 4, :].bitcast(I32).rearrange("r (a w) -> r a w", a=PASSES),
-                    src[32 * q : 32 * q + 32 : 4, :].bitcast(I32),
+                    src[8 * q : 8 * q + 8, :].bitcast(I32),
                 )
 
         def load_words(a):
             nc.sync.dma_start(word_win[a][:], tab_words[a].rearrange("p t i -> p (t i)").bitcast(I32))
+
+        def load_wc(a):
+            raw = kept(f"wc_raw{a}", PACK * H, F32, tag="raw")
+            nc.sync.dma_start(raw[:], wc[512 * a : 512 * (a + 1), :].rearrange("(p j) r -> p (j r)", j=PACK))
+            return raw
 
         def deal(dst, src, run):
             nc.vector.tensor_copy(
@@ -81,38 +79,44 @@ def tile_list_triplex_median_fault_kernel(
             )
 
         nc.sync.dma_start(lists[0][:], offs)
-        load_scale_rows(scale_win[:], tab_scales)
-        load_scale_rows(ws_raw[:, 0:H], wa_scales)
-        load_scale_rows(ws_raw[:, H : 2 * H], wb_scales)
+        load_scale_rows(nc.sync, scale_win[:], tab_scales)
+        load_scale_rows(nc.scalar, ws_raw[:, 0:H], wa_scales)
+        load_scale_rows(nc.scalar, ws_raw[:, H : 2 * H], wb_scales)
+        nc.scalar.dma_start(bias[:], bf.rearrange("(p t) -> p t", t=PACK))
         nc.sync.dma_start(lists[1][:], offs2)
         nc.sync.dma_start(lists[2][:], offs3)
         load_words(0)
-        for a in range(PASSES):
-            nc.sync.dma_start(wc_raw[a][:], wc[512 * a : 512 * (a + 1), :].rearrange("(p j) r -> p (j r)", j=PACK))
         nc.sync.dma_start(
             wa_raw[:].bitcast(I32).rearrange("p (a w) -> p a w", a=PASSES),
             wa_words.bitcast(I32).rearrange("a p w -> p a w"),
         )
-        nc.sync.dma_start(bias[:], bf.rearrange("(p t) -> p t", t=PACK))
+        wc_raw = load_wc(0)
 
-        deal(ws_rows[:].bitcast(I32), ws_raw[:].bitcast(I32), 2)
+        nc.vector.memset(scale_win[32:64, :].bitcast(I32), 0)
+        nc.vector.memset(scale_win[64:P, :].bitcast(I32), 0)
+        nc.vector.memset(w_scales[:].bitcast(I32), 0)
+        nc.vector.memset(picked_scales[:].bitcast(I32), 0)
+
+        deal(ws_rows[0:ROWS, :].bitcast(I32), ws_raw[0:ROWS, :].bitcast(I32), 2)
         place_scale_rows(w_scales[:], ws_rows[:])
-        word_win.append(keep.tile([P, T], I32, name="word_win1", tag="late_words", align_bytes=64))
+        word_win.append(kept("word_win1", T, I32, tag="late_words"))
         load_words(1)
 
         for x in range(3):
             nc.vector.tensor_copy(picked_rows[:, x * S : (x + 1) * S], scale_win[:].indirect(lists[x][:]))
         place_scale_rows(picked_scales[:], picked_rows[:])
-        wb_raw = keep.tile([P, PASSES * H], I32, name="wb_raw", tag="late_wb", align_bytes=64)
+        wb_raw = kept("wb_raw", PASSES * H, I32, tag="late_wb")
         nc.sync.dma_start(
             wb_raw[:].rearrange("p (a w) -> p a w", a=PASSES),
             wb_words.rearrange("a p e i -> a p (e i)").bitcast(I32).rearrange("a p w -> p a w"),
         )
 
         words = {}
+        slot_of = {(1, 0, 1): (0, 1, 0), (2, 0, 0): (0, 1, 1), (2, 0, 1): (1, 1, 0)}
 
         def gather(x, a, half):
-            g = picked.tile([P, HALF], U32, name="g", align_bytes=64)
+            slot = slot_of.get((x, a, half), (x, a, half))
+            g = kept("g%d%d%d" % (x, a, half), HALF, U32, tag="slot%d%d%d" % slot)
             cols = slice(half * HALF // 16, (half + 1) * HALF // 16)
             nc.vector.tensor_copy(g[:], word_win[a][:].bitcast(U32).indirect(lists[x][:, cols]))
             words[x, a, half] = g
@@ -121,6 +125,16 @@ def tile_list_triplex_median_fault_kernel(
         wb_codes = kept("wb_codes", PASSES * H, I32)
         wc_codes = [kept(f"wc_codes{a}", H, U32) for a in range(PASSES)]
         wc_scales = [kept(f"wc_scales{a}", H, U8) for a in range(PASSES)]
+        wc_bf = [kept(f"wc_bf{a}", PACK * H, BF16) for a in range(PASSES)]
+
+        def round_wc(a, raw):
+            dst = wc_bf[a][:].rearrange("p (t q u i j) -> p u q t j i", t=PACK, u=2, i=4, j=PACK)
+            src = raw[:].rearrange("p (j q t u i) -> p u q t j i", t=PACK, u=2, i=4, j=PACK)
+            for u in range(2):
+                nc.scalar.copy(dst[:, u], src[:, u])
+
+        def quantise_wc(a):
+            nc.vector.quantize_mx(out=wc_codes[a][:].bitcast(FP8X4), scales=wc_scales[a][:], in_=wc_bf[a][:])
 
         def stationary(x, a, t):
             lo = a * H + t * P
@@ -132,100 +146,112 @@ def tile_list_triplex_median_fault_kernel(
             return wc_codes[a][:, t * P : (t + 1) * P].bitcast(FP8X4), wc_scales[a][:, t * P : (t + 1) * P]
 
         sums = [[kept(f"sum{x}_{half}", PACK * HALF, BF16) for half in range(2)] for x in range(3)]
+        banks = {}
 
-        def project(x, half):
-            for blk in range(HALF // BLOCK):
-                bank = psum.tile([P, PACK, BLOCK], F32, name=f"bank{half * (HALF // BLOCK) + blk}")
-                j0 = blk * BLOCK
-                for t in range(PACK):
-                    for a in range(PASSES):
-                        codes, scales = stationary(x, a, t)
-                        s0 = (a * 3 + x) * S + half * HALF + j0
-                        nc.tensor.matmul_mx(
-                            out=bank[:, t, :], lhsT=codes, lhsT_scale=scales,
-                            rhs=words[x, a, half][:, j0 : j0 + BLOCK].bitcast(FP8X4),
-                            rhs_scale=picked_scales[:, s0 : s0 + BLOCK],
-                            start=(a == 0), stop=(a == PASSES - 1),
-                        )
-                nc.scalar.copy(
-                    sums[x][half][:, PACK * j0 : PACK * (j0 + BLOCK)].rearrange("p (j t) -> p j t", t=PACK),
-                    bank[:].rearrange("p t j -> p j t"),
+        def multiply(x, a, half, blk):
+            if a == 0:
+                banks[x, half, blk] = psum.tile([P, PACK, BLOCK], F32, name=f"bank{half * BANKS + blk}")
+            bank = banks[x, half, blk]
+            j0 = blk * BLOCK
+            s0 = (a * 3 + x) * S + half * HALF + j0
+            for t in range(PACK):
+                codes, scales = stationary(x, a, t)
+                nc.tensor.matmul_mx(
+                    out=bank[:, t, :], lhsT=codes, lhsT_scale=scales,
+                    rhs=words[x, a, half][:, j0 : j0 + BLOCK].bitcast(FP8X4),
+                    rhs_scale=picked_scales[:, s0 : s0 + BLOCK],
+                    start=(a == 0 and t == 0), stop=(a == PASSES - 1 and t == PACK - 1),
                 )
 
-        for x in range(2):
-            for half in range(2):
-                gather(x, 0, half)
+        def empty(x, half, blk):
+            j0 = blk * BLOCK
+            dst = sums[x][half][:, PACK * j0 : PACK * (j0 + BLOCK)].rearrange("p (j t) -> p j t", t=PACK)
+            src = banks[x, half, blk][:].rearrange("p t j -> p j t")
+            if x == 0:
+                nc.scalar.activation(dst, src, IDENTITY)
+            else:
+                nc.scalar.copy(dst, src)
 
-        wc_bf = [kept(f"wc_bf{a}", PACK * H, BF16) for a in range(PASSES)]
-        for a in range(PASSES):
-            dst = wc_bf[a][:].rearrange("p (t q u i j) -> p u q t j i", t=PACK, u=2, i=4, j=PACK)
-            src = wc_raw[a][:].rearrange("p (j q t u i) -> p u q t j i", t=PACK, u=2, i=4, j=PACK)
-            for u in range(2):
-                nc.scalar.copy(dst[:, u], src[:, u])
-        wf_raw = stage.tile([P, PACK * N], F32, name="raw", align_bytes=64)
+        def project(x, half):
+            for blk in range(BANKS):
+                for a in range(PASSES):
+                    multiply(x, a, half, blk)
+                empty(x, half, blk)
+
+        deal(wa_codes[:].bitcast(I32), wa_raw[:].bitcast(I32), 4)
+        round_wc(0, wc_raw)
+        wc_raw = load_wc(1)
+        for half in range(2):
+            gather(0, 0, half)
+            for blk in range(BANKS):
+                multiply(0, 0, half, blk)
+        gather(1, 0, 0)
+        quantise_wc(0)
+        for half in range(2):
+            gather(0, 1, half)
+            for blk in range(BANKS):
+                multiply(0, 1, half, blk)
+                empty(0, half, blk)
+        round_wc(1, wc_raw)
+        wf_raw = kept("wf_raw", PACK * N, F32, tag="raw")
         wf_rows = wf.rearrange("(q t i) n -> t q i n", t=PACK, i=8)
         for t in range(PACK):
             nc.sync.dma_start(wf_raw[:, t * N : (t + 1) * N], wf_rows[t])
-        deal(wa_codes[:].bitcast(I32), wa_raw[:].bitcast(I32), 4)
-        for half in range(2):
-            gather(0, 1, half)
-            project(0, half)
         deal(wb_codes[:], wb_raw[:], 8)
-        for half in range(2):
-            gather(1, 1, half)
-            project(1, half)
+        gather(1, 1, 0)
+        project(1, 0)
         for a in range(PASSES):
-            nc.vector.quantize_mx(out=wc_codes[a][:].bitcast(FP8X4), scales=wc_scales[a][:], in_=wc_bf[a][:])
-        for half in range(2):
-            for a in range(PASSES):
-                gather(2, a, half)
-            project(2, half)
-
+            gather(1, a, 1)
+        project(1, 1)
+        quantise_wc(1)
+        for a in range(PASSES):
+            gather(2, a, 0)
         wf_bf = kept("wf_bf", PACK * N, BF16)
         nc.scalar.copy(
             wf_bf[:].rearrange("p (t m j) -> p m j t", t=PACK, j=PACK),
             wf_raw[:].rearrange("p (j m t) -> p m j t", t=PACK, j=PACK),
         )
+        project(2, 0)
+        for a in range(PASSES):
+            gather(2, a, 1)
+        project(2, 1)
+
+        highs = [kept(f"high{half}", PACK * HALF, BF16) for half in range(2)]
+        lows = [kept(f"low{half}", PACK * HALF, BF16) for half in range(2)]
+
+        def bounds(half):
+            nc.vector.tensor_tensor(highs[half][:], sums[0][half][:], sums[1][half][:], MAX)
+            nc.vector.tensor_tensor(lows[half][:], sums[0][half][:], sums[1][half][:], MIN)
+
         wf_codes = kept("wf_codes", N, U32)
         wf_scales = kept("wf_scales", N, U8)
-        nc.vector.quantize_mx(out=wf_codes[:].bitcast(FP8X4), scales=wf_scales[:], in_=wf_bf[:])
-
         y_scales = kept("y_scales", S, U8)
         y_rows = out_0.rearrange("(p t) j -> p t j", t=PACK)
         y_words = out_1[0].rearrange("p m i -> p (m i)").bitcast(I32)
-        last = len(CHUNKS) - 1
         state = {}
 
-        def part(x, c):
-            j0, width = CHUNKS[c]
-            half, off = divmod(j0, HALF)
-            return sums[x][half][:, PACK * off : PACK * (off + width)]
-
-        def pick(name, c, in0, in1, op):
-            out = work.tile([P, PACK * CHUNKS[c][1]], BF16, name=name, align_bytes=64)
-            nc.vector.tensor_tensor(out[:], in0, in1, op)
-            state[name, c] = out[:]
-
-        def high(c):
-            pick("high", c, part(0, c), part(1, c), MAX)
-
-        def low(c):
-            pick("low", c, part(0, c), part(1, c), MIN)
+        def part(tiles, c):
+            half, off = divmod(c * CHUNK, HALF)
+            return tiles[half][:, PACK * off : PACK * (off + CHUNK)]
 
         def clip(c):
-            pick("clip", c, state["high", c], part(2, c), MIN)
+            out = work.tile([P, PACK * CHUNK], BF16, name="clipped", align_bytes=64)
+            nc.vector.tensor_tensor(out[:], part(highs, c), part(sums[2], c), MIN)
+            state["clip", c] = out
 
         def median(c):
-            pick("median", c, state["low", c], state["clip", c], MAX)
+            out = work.tile([P, PACK * CHUNK], BF16, name="median", align_bytes=64)
+            nc.vector.tensor_tensor(out[:], part(lows, c), state["clip", c][:], MAX)
+            state["median", c] = out
 
         def score(c):
-            j0, width = CHUNKS[c]
-            h_codes = work.tile([P, width], U32, name="h_codes", align_bytes=64)
-            h_scales = work.tile([P, width], U8, name="h_scales", align_bytes=64)
-            nc.vector.quantize_mx(out=h_codes[:].bitcast(FP8X4), scales=h_scales[:], in_=state["median", c])
-            y = kept(f"y{c}", PACK * width, F32)
+            j0 = c * CHUNK
+            h_codes = kept(f"h_codes{c}", CHUNK, U32)
+            h_scales = kept(f"h_scales{c}", CHUNK, U8)
+            nc.vector.quantize_mx(out=h_codes[:].bitcast(FP8X4), scales=h_scales[:], in_=state["median", c][:])
+            y = kept(f"y{c}", PACK * CHUNK, F32)
             for pair in range(2):
-                bank = psum.tile([P, 2, width], F32, name=f"bank{7 - pair}")
+                bank = psum.tile([P, 2, CHUNK], F32, name=f"bank{2 * (c % 2) + pair}")
                 for u in range(2):
                     t = 2 * pair + u
                     nc.tensor.matmul_mx(
@@ -236,14 +262,14 @@ def tile_list_triplex_median_fault_kernel(
                 for u in range(2):
                     t = 2 * pair + u
                     nc.scalar.activation(
-                        y[:, t * width : (t + 1) * width], bank[:, u, :], IDENTITY, bias=bias[:, t : t + 1]
+                        y[:, t * CHUNK : (t + 1) * CHUNK], bank[:, u, :], IDENTITY, bias=bias[:, t : t + 1]
                     )
-            nc.sync.dma_start(y_rows[:, :, j0 : j0 + width], y[:].rearrange("p (t j) -> p t j", t=PACK))
+            nc.sync.dma_start(y_rows[:, :, j0 : j0 + CHUNK], y[:].rearrange("p (t j) -> p t j", t=PACK))
             state["y", c] = y
 
         def weave(c):
-            y_bf = kept(f"y_bf{c}", PACK * CHUNKS[c][1], BF16)
-            copy = nc.vector.tensor_copy if c >= last - 1 else nc.scalar.copy
+            y_bf = kept(f"y_bf{c}", PACK * CHUNK, BF16)
+            copy = nc.scalar.copy if c in SCALAR_WEAVES else nc.vector.tensor_copy
             copy(
                 y_bf[:].rearrange("p (c i t) -> p c t i", t=PACK, i=4),
                 state["y", c][:].rearrange("p (t c i) -> p c t i", t=PACK, i=4),
@@ -251,31 +277,24 @@ def tile_list_triplex_median_fault_kernel(
             state["y_bf", c] = y_bf
 
         def planes(c):
-            j0, width = CHUNKS[c]
-            y_codes = kept(f"y_codes{c}", width, U32)
+            j0 = c * CHUNK
+            y_codes = kept(f"y_codes{c}", CHUNK, U32)
             nc.vector.quantize_mx(
-                out=y_codes[:].bitcast(FP8X4), scales=y_scales[:, j0 : j0 + width], in_=state["y_bf", c][:]
+                out=y_codes[:].bitcast(FP8X4), scales=y_scales[:, j0 : j0 + CHUNK], in_=state["y_bf", c][:]
             )
-            nc.sync.dma_start(y_words[:, j0 : j0 + width], y_codes[:].bitcast(I32))
+            nc.sync.dma_start(y_words[:, j0 : j0 + CHUNK], y_codes[:].bitcast(I32))
 
-        high(0)
-        low(0)
-        for c in range(len(CHUNKS)):
-            clip(c)
-            if c < last:
-                high(c + 1)
-            median(c)
-            if c < last:
-                low(c + 1)
-            if c >= 2:
-                planes(c - 2)
-            score(c)
-            if c < last - 1:
-                weave(c)
-        weave(last - 1)
-        weave(last)
-        planes(last - 1)
-        planes(last)
+        bounds(0)
+        bounds(1)
+        nc.vector.quantize_mx(out=wf_codes[:].bitcast(FP8X4), scales=wf_scales[:], in_=wf_bf[:])
+        for c in range(0, CHUNKS, 2):
+            for step in (clip, median, score):
+                step(c)
+                step(c + 1)
+        for c in range(0, CHUNKS, 2):
+            for step in (weave, planes):
+                step(c)
+                step(c + 1)
         for q in range(QUADS):
             eng = nc.scalar if q % 2 else nc.sync
             eng.dma_start(out_2[0, 4 * q : 4 * q + 4, :].bitcast(I32), y_scales[32 * q : 32 * q + 4, :].bitcast(I32))

@@ -23,11 +23,11 @@ PASSES = K // (P * PACK)
 HALF = S // 2
 BLOCK = 128
 BANKS = HALF // BLOCK
-CHUNK = 256
-CHUNKS = S // CHUNK
+CHUNKS = ((0, 256), (256, 256), (512, 256), (768, 128), (896, 128))
 QUADS = 4
 ROWS = 32
-SCALAR_WEAVES = ()
+FIRST = 2 * H + S
+SCALAR_WEAVES = (0, 1)
 
 
 def tile_list_triplex_median_fault_kernel(
@@ -37,22 +37,26 @@ def tile_list_triplex_median_fault_kernel(
     nc = tc.nc
     with ExitStack() as ctx:
         keep = ctx.enter_context(tc.tile_pool(name="keep", bufs=1))
-        work = ctx.enter_context(tc.tile_pool(name="work", bufs=2))
+        late = ctx.enter_context(tc.tile_pool(name="late", bufs=1))
         psum = ctx.enter_context(tc.psum_pool(name="psum", bufs=1))
 
         def kept(name, width, dtype, tag=None):
             return keep.tile([P, width], dtype, name=name, tag=tag or name, align_bytes=64)
 
+        def placed(name, width, dtype, offset):
+            return late.tile([P, width], dtype, name=name, offset=offset, align_bytes=64)
+
         lists = [keep.tile([P, S // 16], U16, name=f"list{x}") for x in range(3)]
         scale_win = kept("scale_win", T, U8)
         word_win = [kept("word_win0", T, I32)]
-        wa_raw = kept("wa_raw", PASSES * 2 * H, U8)
+        wa_raw = placed("wa_raw", PASSES * 2 * H, U8, 7168)
         ws_raw = kept("ws_raw", 2 * H, U8)
-        ws_rows = kept("ws_rows", 2 * H, U8, tag="late_words")
-        w_scales = kept("w_scales", PASSES * 2 * H, U8)
+        first_rows = kept("first_rows", FIRST, U8, tag="late_wb")
+        first_scales = kept("first_scales", PASSES * FIRST, U8)
         bias = kept("bias", PACK, F32)
-        picked_rows = kept("picked_rows", 3 * S, U8, tag="late_wb")
-        picked_scales = kept("picked_scales", PASSES * 3 * S, U8)
+        a_rows = kept("a_rows", S, U8, tag="wa_codes")
+        bc_rows = placed("bc_rows", 2 * S, U8, 6144)
+        bc_scales = kept("bc_scales", PASSES * 2 * S, U8)
 
         def load_scale_rows(eng, dst, src):
             eng.dma_start(dst[0:ROWS, :].bitcast(I32), src.rearrange("a q t -> q a t").bitcast(I32))
@@ -82,29 +86,32 @@ def tile_list_triplex_median_fault_kernel(
         load_scale_rows(nc.sync, scale_win[:], tab_scales)
         load_scale_rows(nc.scalar, ws_raw[:, 0:H], wa_scales)
         load_scale_rows(nc.scalar, ws_raw[:, H : 2 * H], wb_scales)
-        nc.scalar.dma_start(bias[:], bf.rearrange("(p t) -> p t", t=PACK))
         nc.sync.dma_start(lists[1][:], offs2)
         nc.sync.dma_start(lists[2][:], offs3)
-        load_words(0)
         nc.sync.dma_start(
             wa_raw[:].bitcast(I32).rearrange("p (a w) -> p a w", a=PASSES),
             wa_words.bitcast(I32).rearrange("a p w -> p a w"),
         )
+        load_words(0)
+        nc.scalar.dma_start(bias[:], bf.rearrange("(p t) -> p t", t=PACK))
         wc_raw = load_wc(0)
 
         nc.vector.memset(scale_win[32:64, :].bitcast(I32), 0)
         nc.vector.memset(scale_win[64:P, :].bitcast(I32), 0)
-        nc.vector.memset(w_scales[:].bitcast(I32), 0)
-        nc.vector.memset(picked_scales[:].bitcast(I32), 0)
+        nc.vector.memset(first_scales[:].bitcast(I32), 0)
+        nc.gpsimd.memset(bc_scales[:].bitcast(I32), 0)
 
-        deal(ws_rows[0:ROWS, :].bitcast(I32), ws_raw[0:ROWS, :].bitcast(I32), 2)
-        place_scale_rows(w_scales[:], ws_rows[:])
-        word_win.append(kept("word_win1", T, I32, tag="late_words"))
+        nc.vector.tensor_copy(a_rows[:], scale_win[:].indirect(lists[0][:]))
+        deal(first_rows[0:ROWS, 0 : 2 * H].bitcast(I32), ws_raw[0:ROWS, :].bitcast(I32), 2)
+        nc.vector.tensor_copy(first_rows[0:ROWS, 2 * H : FIRST].bitcast(I32), a_rows[0:ROWS, :].bitcast(I32))
+        place_scale_rows(first_scales[:], first_rows[:])
+        wa_codes = kept("wa_codes", PASSES * 2 * H, U8)
+        deal(wa_codes[:].bitcast(I32), wa_raw[:].bitcast(I32), 4)
+        word_win.append(placed("word_win1", T, I32, 8192))
         load_words(1)
-
-        for x in range(3):
-            nc.vector.tensor_copy(picked_rows[:, x * S : (x + 1) * S], scale_win[:].indirect(lists[x][:]))
-        place_scale_rows(picked_scales[:], picked_rows[:])
+        for x in range(1, 3):
+            nc.vector.tensor_copy(bc_rows[:, (x - 1) * S : x * S], scale_win[:].indirect(lists[x][:]))
+        place_scale_rows(bc_scales[:], bc_rows[:])
         wb_raw = kept("wb_raw", PASSES * H, I32, tag="late_wb")
         nc.sync.dma_start(
             wb_raw[:].rearrange("p (a w) -> p a w", a=PASSES),
@@ -121,7 +128,6 @@ def tile_list_triplex_median_fault_kernel(
             nc.vector.tensor_copy(g[:], word_win[a][:].bitcast(U32).indirect(lists[x][:, cols]))
             words[x, a, half] = g
 
-        wa_codes = kept("wa_codes", PASSES * 2 * H, U8)
         wb_codes = kept("wb_codes", PASSES * H, I32)
         wc_codes = [kept(f"wc_codes{a}", H, U32) for a in range(PASSES)]
         wc_scales = [kept(f"wc_scales{a}", H, U8) for a in range(PASSES)]
@@ -138,11 +144,11 @@ def tile_list_triplex_median_fault_kernel(
 
         def stationary(x, a, t):
             lo = a * H + t * P
-            s0 = (2 * a + x) * H + t * P
+            s0 = a * FIRST + x * H + t * P
             if x == 0:
-                return wa_codes[:, 2 * lo : 2 * (lo + P)].bitcast(FP4X4), w_scales[:, s0 : s0 + P]
+                return wa_codes[:, 2 * lo : 2 * (lo + P)].bitcast(FP4X4), first_scales[:, s0 : s0 + P]
             if x == 1:
-                return wb_codes[:, lo : lo + P].bitcast(FP8X4), w_scales[:, s0 : s0 + P]
+                return wb_codes[:, lo : lo + P].bitcast(FP8X4), first_scales[:, s0 : s0 + P]
             return wc_codes[a][:, t * P : (t + 1) * P].bitcast(FP8X4), wc_scales[a][:, t * P : (t + 1) * P]
 
         sums = [[kept(f"sum{x}_{half}", PACK * HALF, BF16) for half in range(2)] for x in range(3)]
@@ -153,13 +159,14 @@ def tile_list_triplex_median_fault_kernel(
                 banks[x, half, blk] = psum.tile([P, PACK, BLOCK], F32, name=f"bank{half * BANKS + blk}")
             bank = banks[x, half, blk]
             j0 = blk * BLOCK
-            s0 = (a * 3 + x) * S + half * HALF + j0
+            s0 = half * HALF + j0 + (a * FIRST + 2 * H if x == 0 else (2 * a + x - 1) * S)
+            plane = first_scales if x == 0 else bc_scales
             for t in range(PACK):
                 codes, scales = stationary(x, a, t)
                 nc.tensor.matmul_mx(
                     out=bank[:, t, :], lhsT=codes, lhsT_scale=scales,
                     rhs=words[x, a, half][:, j0 : j0 + BLOCK].bitcast(FP8X4),
-                    rhs_scale=picked_scales[:, s0 : s0 + BLOCK],
+                    rhs_scale=plane[:, s0 : s0 + BLOCK],
                     start=(a == 0 and t == 0), stop=(a == PASSES - 1 and t == PACK - 1),
                 )
 
@@ -178,9 +185,12 @@ def tile_list_triplex_median_fault_kernel(
                     multiply(x, a, half, blk)
                 empty(x, half, blk)
 
-        deal(wa_codes[:].bitcast(I32), wa_raw[:].bitcast(I32), 4)
         round_wc(0, wc_raw)
         wc_raw = load_wc(1)
+        wf_raw = placed("wf_raw", PACK * N, F32, 0)
+        wf_rows = wf.rearrange("(q t i) n -> t q i n", t=PACK, i=8)
+        for t in range(PACK):
+            nc.sync.dma_start(wf_raw[:, t * N : (t + 1) * N], wf_rows[t])
         for half in range(2):
             gather(0, 0, half)
             for blk in range(BANKS):
@@ -193,10 +203,6 @@ def tile_list_triplex_median_fault_kernel(
                 multiply(0, 1, half, blk)
                 empty(0, half, blk)
         round_wc(1, wc_raw)
-        wf_raw = kept("wf_raw", PACK * N, F32, tag="raw")
-        wf_rows = wf.rearrange("(q t i) n -> t q i n", t=PACK, i=8)
-        for t in range(PACK):
-            nc.sync.dma_start(wf_raw[:, t * N : (t + 1) * N], wf_rows[t])
         deal(wb_codes[:], wb_raw[:], 8)
         gather(1, 1, 0)
         project(1, 0)
@@ -208,8 +214,8 @@ def tile_list_triplex_median_fault_kernel(
             gather(2, a, 0)
         wf_bf = kept("wf_bf", PACK * N, BF16)
         nc.scalar.copy(
-            wf_bf[:].rearrange("p (t m j) -> p m j t", t=PACK, j=PACK),
-            wf_raw[:].rearrange("p (j m t) -> p m j t", t=PACK, j=PACK),
+            wf_bf[:].rearrange("p (t m j) -> p m t j", t=PACK, j=PACK),
+            wf_raw[:].rearrange("p (j m t) -> p m t j", t=PACK, j=PACK),
         )
         project(2, 0)
         for a in range(PASSES):
@@ -218,40 +224,44 @@ def tile_list_triplex_median_fault_kernel(
 
         highs = [kept(f"high{half}", PACK * HALF, BF16) for half in range(2)]
         lows = [kept(f"low{half}", PACK * HALF, BF16) for half in range(2)]
-
-        def bounds(half):
-            nc.vector.tensor_tensor(highs[half][:], sums[0][half][:], sums[1][half][:], MAX)
-            nc.vector.tensor_tensor(lows[half][:], sums[0][half][:], sums[1][half][:], MIN)
-
+        clips = [kept(f"clip{half}", PACK * HALF, BF16) for half in range(2)]
+        medians = [kept(f"median{half}", PACK * HALF, BF16) for half in range(2)]
         wf_codes = kept("wf_codes", N, U32)
         wf_scales = kept("wf_scales", N, U8)
+        y_bf = [kept(f"y_bf{half}", PACK * HALF, BF16) for half in range(2)]
+        y_codes = [kept(f"y_codes{half}", HALF, U32) for half in range(2)]
         y_scales = kept("y_scales", S, U8)
         y_rows = out_0.rearrange("(p t) j -> p t j", t=PACK)
         y_words = out_1[0].rearrange("p m i -> p (m i)").bitcast(I32)
         state = {}
 
-        def part(tiles, c):
-            half, off = divmod(c * CHUNK, HALF)
-            return tiles[half][:, PACK * off : PACK * (off + CHUNK)]
+        def part(tiles, j0, width):
+            half, off = divmod(j0, HALF)
+            return tiles[half][:, PACK * off : PACK * (off + width)]
 
-        def clip(c):
-            out = work.tile([P, PACK * CHUNK], BF16, name="clipped", align_bytes=64)
-            nc.vector.tensor_tensor(out[:], part(highs, c), part(sums[2], c), MIN)
-            state["clip", c] = out
+        def pick(out, in0, in1, op, j0, width):
+            nc.vector.tensor_tensor(part(out, j0, width), part(in0, j0, width), part(in1, j0, width), op)
 
-        def median(c):
-            out = work.tile([P, PACK * CHUNK], BF16, name="median", align_bytes=64)
-            nc.vector.tensor_tensor(out[:], part(lows, c), state["clip", c][:], MAX)
-            state["median", c] = out
+        def high(j0, width):
+            pick(highs, sums[0], sums[1], MAX, j0, width)
+
+        def low(j0, width):
+            pick(lows, sums[0], sums[1], MIN, j0, width)
+
+        def clip(j0, width):
+            pick(clips, highs, sums[2], MIN, j0, width)
+
+        def median(j0, width):
+            pick(medians, lows, clips, MAX, j0, width)
 
         def score(c):
-            j0 = c * CHUNK
-            h_codes = kept(f"h_codes{c}", CHUNK, U32)
-            h_scales = kept(f"h_scales{c}", CHUNK, U8)
-            nc.vector.quantize_mx(out=h_codes[:].bitcast(FP8X4), scales=h_scales[:], in_=state["median", c][:])
-            y = kept(f"y{c}", PACK * CHUNK, F32)
+            j0, width = CHUNKS[c]
+            h_codes = kept(f"h_codes{c}", width, U32)
+            h_scales = kept(f"h_scales{c}", width, U8)
+            nc.vector.quantize_mx(out=h_codes[:].bitcast(FP8X4), scales=h_scales[:], in_=part(medians, j0, width))
+            y = kept(f"y{c}", PACK * width, F32)
             for pair in range(2):
-                bank = psum.tile([P, 2, CHUNK], F32, name=f"bank{2 * (c % 2) + pair}")
+                bank = psum.tile([P, 2, width], F32, name=f"bank{2 * (c % 2) + pair}")
                 for u in range(2):
                     t = 2 * pair + u
                     nc.tensor.matmul_mx(
@@ -262,39 +272,56 @@ def tile_list_triplex_median_fault_kernel(
                 for u in range(2):
                     t = 2 * pair + u
                     nc.scalar.activation(
-                        y[:, t * CHUNK : (t + 1) * CHUNK], bank[:, u, :], IDENTITY, bias=bias[:, t : t + 1]
+                        y[:, t * width : (t + 1) * width], bank[:, u, :], IDENTITY, bias=bias[:, t : t + 1]
                     )
-            nc.sync.dma_start(y_rows[:, :, j0 : j0 + CHUNK], y[:].rearrange("p (t j) -> p t j", t=PACK))
+            nc.sync.dma_start(y_rows[:, :, j0 : j0 + width], y[:].rearrange("p (t j) -> p t j", t=PACK))
             state["y", c] = y
 
         def weave(c):
-            y_bf = kept(f"y_bf{c}", PACK * CHUNK, BF16)
             copy = nc.scalar.copy if c in SCALAR_WEAVES else nc.vector.tensor_copy
             copy(
-                y_bf[:].rearrange("p (c i t) -> p c t i", t=PACK, i=4),
+                part(y_bf, *CHUNKS[c]).rearrange("p (c i t) -> p c t i", t=PACK, i=4),
                 state["y", c][:].rearrange("p (t c i) -> p c t i", t=PACK, i=4),
             )
-            state["y_bf", c] = y_bf
 
-        def planes(c):
-            j0 = c * CHUNK
-            y_codes = kept(f"y_codes{c}", CHUNK, U32)
+        def planes(j0, width):
+            half, off = divmod(j0, HALF)
             nc.vector.quantize_mx(
-                out=y_codes[:].bitcast(FP8X4), scales=y_scales[:, j0 : j0 + CHUNK], in_=state["y_bf", c][:]
+                out=y_codes[half][:, off : off + width].bitcast(FP8X4), scales=y_scales[:, j0 : j0 + width],
+                in_=part(y_bf, j0, width),
             )
-            nc.sync.dma_start(y_words[:, j0 : j0 + CHUNK], y_codes[:].bitcast(I32))
+            if off + width == HALF:
+                nc.sync.dma_start(y_words[:, half * HALF : (half + 1) * HALF], y_codes[half][:].bitcast(I32))
 
-        bounds(0)
-        bounds(1)
+        high(0, HALF)
+        low(0, HALF)
         nc.vector.quantize_mx(out=wf_codes[:].bitcast(FP8X4), scales=wf_scales[:], in_=wf_bf[:])
-        for c in range(0, CHUNKS, 2):
-            for step in (clip, median, score):
-                step(c)
-                step(c + 1)
-        for c in range(0, CHUNKS, 2):
-            for step in (weave, planes):
-                step(c)
-                step(c + 1)
+        for step in (clip, median):
+            step(*CHUNKS[0])
+            step(*CHUNKS[1])
+        score(0)
+        score(1)
+        weave(0)
+        weave(1)
+        third, fourth = (512, 256), (768, 256)
+        high(*third)
+        low(*third)
+        clip(*third)
+        high(*fourth)
+        median(*third)
+        low(*fourth)
+        score(2)
+        clip(*fourth)
+        planes(*CHUNKS[0])
+        median(*fourth)
+        planes(*CHUNKS[1])
+        score(3)
+        score(4)
+        weave(2)
+        weave(3)
+        planes(*third)
+        weave(4)
+        planes(*fourth)
         for q in range(QUADS):
             eng = nc.scalar if q % 2 else nc.sync
             eng.dma_start(out_2[0, 4 * q : 4 * q + 4, :].bitcast(I32), y_scales[32 * q : 32 * q + 4, :].bitcast(I32))

@@ -27,7 +27,7 @@ CHUNKS = ((0, 256), (256, 256), (512, 256), (768, 128), (896, 128))
 QUADS = 4
 ROWS = 32
 FIRST = 2 * H + S
-SCALAR_WEAVES = (0, 1)
+SCALAR_WEAVES = ()
 
 
 def tile_list_triplex_median_fault_kernel(
@@ -172,8 +172,8 @@ def tile_list_triplex_median_fault_kernel(
 
         def empty(x, half, blk):
             j0 = blk * BLOCK
-            dst = sums[x][half][:, PACK * j0 : PACK * (j0 + BLOCK)].rearrange("p (j t) -> p j t", t=PACK)
-            src = banks[x, half, blk][:].rearrange("p t j -> p j t")
+            dst = sums[x][half][:, PACK * j0 : PACK * (j0 + BLOCK)].rearrange("p (c i t) -> p c t i", t=PACK, i=4)
+            src = banks[x, half, blk][:].rearrange("p t (c i) -> p c t i", i=4)
             if x == 0:
                 nc.scalar.activation(dst, src, IDENTITY)
             else:
@@ -214,8 +214,8 @@ def tile_list_triplex_median_fault_kernel(
             gather(2, a, 0)
         wf_bf = kept("wf_bf", PACK * N, BF16)
         nc.scalar.copy(
-            wf_bf[:].rearrange("p (t m j) -> p m t j", t=PACK, j=PACK),
-            wf_raw[:].rearrange("p (j m t) -> p m t j", t=PACK, j=PACK),
+            wf_bf[:].rearrange("p (t m j) -> p m j t", t=PACK, j=PACK),
+            wf_raw[:].rearrange("p (j m t) -> p m j t", t=PACK, j=PACK),
         )
         project(2, 0)
         for a in range(PASSES):

@@ -48,15 +48,14 @@ def tile_list_triplex_median_fault_kernel(
 
         lists = [keep.tile([P, S // 16], U16, name=f"list{x}") for x in range(3)]
         scale_win = kept("scale_win", T, U8)
-        word_win = [kept("word_win0", T, I32)]
-        wa_raw = placed("wa_raw", PASSES * 2 * H, U8, 7168)
+        word_win = [kept(f"word_win{a}", T, I32) for a in range(PASSES)]
+        wa_raw = kept("wa_raw", PASSES * 2 * H, U8)[:]
         ws_raw = kept("ws_raw", 2 * H, U8)
-        first_rows = kept("first_rows", FIRST, U8, tag="late_wb")
+        first_rows = kept("first_rows", FIRST, U8)
         first_scales = kept("first_scales", PASSES * FIRST, U8)
         bias = kept("bias", PACK, F32)
-        a_rows = kept("a_rows", S, U8, tag="wa_codes")
-        bc_rows = placed("bc_rows", 2 * S, U8, 6144)
-        bc_scales = kept("bc_scales", PASSES * 2 * S, U8)
+        a_rows = kept("a_rows", S, U8)
+        bc_rows = kept("bc_rows", 2 * S, U8)
 
         def load_scale_rows(eng, dst, src):
             eng.dma_start(dst[0:ROWS, :].bitcast(I32), src.rearrange("a q t -> q a t").bitcast(I32))
@@ -72,7 +71,7 @@ def tile_list_triplex_median_fault_kernel(
             nc.sync.dma_start(word_win[a][:], tab_words[a].rearrange("p t i -> p (t i)").bitcast(I32))
 
         def load_wc(a):
-            raw = kept(f"wc_raw{a}", PACK * H, F32, tag="raw")
+            raw = kept(f"wc_raw{a}", PACK * H, F32)
             nc.sync.dma_start(raw[:], wc[512 * a : 512 * (a + 1), :].rearrange("(p j) r -> p (j r)", j=PACK))
             return raw
 
@@ -82,6 +81,14 @@ def tile_list_triplex_median_fault_kernel(
                 src.rearrange("p (a q t w) -> p a t q w", a=2, t=PACK, w=run),
             )
 
+        wc_bf = [kept("wc_bf0", PACK * H, BF16), placed("wc_bf1", PACK * H, BF16, 4096)]
+
+        def round_wc(a):
+            dst = wc_bf[a][:].rearrange("p (t q u i j) -> p u q t j i", t=PACK, u=2, i=4, j=PACK)
+            src = wc_raw[a][:].rearrange("p (j q t u i) -> p u q t j i", t=PACK, u=2, i=4, j=PACK)
+            for u in range(2):
+                nc.scalar.copy(dst[:, u], src[:, u])
+
         nc.sync.dma_start(lists[0][:], offs)
         load_scale_rows(nc.sync, scale_win[:], tab_scales)
         load_scale_rows(nc.scalar, ws_raw[:, 0:H], wa_scales)
@@ -89,41 +96,44 @@ def tile_list_triplex_median_fault_kernel(
         nc.sync.dma_start(lists[1][:], offs2)
         nc.sync.dma_start(lists[2][:], offs3)
         nc.sync.dma_start(
-            wa_raw[:].bitcast(I32).rearrange("p (a w) -> p a w", a=PASSES),
+            wa_raw.bitcast(I32).rearrange("p (a w) -> p a w", a=PASSES),
             wa_words.bitcast(I32).rearrange("a p w -> p a w"),
         )
         load_words(0)
-        nc.scalar.dma_start(bias[:], bf.rearrange("(p t) -> p t", t=PACK))
-        wc_raw = load_wc(0)
+        wc_raw = [load_wc(a) for a in range(PASSES)]
+        load_words(1)
+        wb_raw = placed("wb_raw", PASSES * H, I32, 0)
+        nc.sync.dma_start(
+            wb_raw[:].rearrange("p (a w) -> p a w", a=PASSES),
+            wb_words.rearrange("a p e i -> a p (e i)").bitcast(I32).rearrange("a p w -> p a w"),
+        )
+        nc.sync.dma_start(bias[:], bf.rearrange("(p t) -> p t", t=PACK))
 
         nc.vector.memset(scale_win[32:64, :].bitcast(I32), 0)
         nc.vector.memset(scale_win[64:P, :].bitcast(I32), 0)
-        nc.vector.memset(first_scales[:].bitcast(I32), 0)
-        nc.gpsimd.memset(bc_scales[:].bitcast(I32), 0)
 
         nc.vector.tensor_copy(a_rows[:], scale_win[:].indirect(lists[0][:]))
         deal(first_rows[0:ROWS, 0 : 2 * H].bitcast(I32), ws_raw[0:ROWS, :].bitcast(I32), 2)
         nc.vector.tensor_copy(first_rows[0:ROWS, 2 * H : FIRST].bitcast(I32), a_rows[0:ROWS, :].bitcast(I32))
         place_scale_rows(first_scales[:], first_rows[:])
         wa_codes = kept("wa_codes", PASSES * 2 * H, U8)
-        deal(wa_codes[:].bitcast(I32), wa_raw[:].bitcast(I32), 4)
-        word_win.append(placed("word_win1", T, I32, 8192))
-        load_words(1)
+        deal(wa_codes[:].bitcast(I32), wa_raw.bitcast(I32), 4)
         for x in range(1, 3):
             nc.vector.tensor_copy(bc_rows[:, (x - 1) * S : x * S], scale_win[:].indirect(lists[x][:]))
+        for a in range(PASSES):
+            round_wc(a)
+        bc_scales = kept("bc_scales", PASSES * 2 * S, U8, tag="wc_raw1")
         place_scale_rows(bc_scales[:], bc_rows[:])
-        wb_raw = kept("wb_raw", PASSES * H, I32, tag="late_wb")
-        nc.sync.dma_start(
-            wb_raw[:].rearrange("p (a w) -> p a w", a=PASSES),
-            wb_words.rearrange("a p e i -> a p (e i)").bitcast(I32).rearrange("a p w -> p a w"),
-        )
 
         words = {}
-        slot_of = {(1, 0, 1): (0, 1, 0), (2, 0, 0): (0, 1, 1), (2, 0, 1): (1, 1, 0)}
+        after = {(2, 0, 1): 0, (2, 1, 1): 2048, (1, 0, 0): 4096, (1, 1, 1): 6144}
 
         def gather(x, a, half):
-            slot = slot_of.get((x, a, half), (x, a, half))
-            g = kept("g%d%d%d" % (x, a, half), HALF, U32, tag="slot%d%d%d" % slot)
+            name = "g%d%d%d" % (x, a, half)
+            if (x, a, half) in after:
+                g = placed(name, HALF, U32, after[x, a, half])
+            else:
+                g = kept(name, HALF, U32, tag="g011" if name == "g101" else None)
             cols = slice(half * HALF // 16, (half + 1) * HALF // 16)
             nc.vector.tensor_copy(g[:], word_win[a][:].bitcast(U32).indirect(lists[x][:, cols]))
             words[x, a, half] = g
@@ -131,14 +141,6 @@ def tile_list_triplex_median_fault_kernel(
         wb_codes = kept("wb_codes", PASSES * H, I32)
         wc_codes = [kept(f"wc_codes{a}", H, U32) for a in range(PASSES)]
         wc_scales = [kept(f"wc_scales{a}", H, U8) for a in range(PASSES)]
-        wc_bf = [kept(f"wc_bf{a}", PACK * H, BF16) for a in range(PASSES)]
-
-        def round_wc(a, raw):
-            dst = wc_bf[a][:].rearrange("p (t q u i j) -> p u q t j i", t=PACK, u=2, i=4, j=PACK)
-            src = raw[:].rearrange("p (j q t u i) -> p u q t j i", t=PACK, u=2, i=4, j=PACK)
-            for u in range(2):
-                nc.scalar.copy(dst[:, u], src[:, u])
-
         def quantise_wc(a):
             nc.vector.quantize_mx(out=wc_codes[a][:].bitcast(FP8X4), scales=wc_scales[a][:], in_=wc_bf[a][:])
 
@@ -156,7 +158,7 @@ def tile_list_triplex_median_fault_kernel(
 
         def multiply(x, a, half, blk):
             if a == 0:
-                banks[x, half, blk] = psum.tile([P, PACK, BLOCK], F32, name=f"bank{half * BANKS + blk}")
+                banks[x, half, blk] = psum.tile([P, PACK, BLOCK], F32, name=f"bank{(half, 1, 0)[x] * BANKS + blk}")
             bank = banks[x, half, blk]
             j0 = blk * BLOCK
             s0 = half * HALF + j0 + (a * FIRST + 2 * H if x == 0 else (2 * a + x - 1) * S)
@@ -185,42 +187,41 @@ def tile_list_triplex_median_fault_kernel(
                     multiply(x, a, half, blk)
                 empty(x, half, blk)
 
-        round_wc(0, wc_raw)
-        wc_raw = load_wc(1)
-        wf_raw = placed("wf_raw", PACK * N, F32, 0)
+        wf_raw = kept("wf_raw", PACK * N, F32, tag="wc_raw0")
         wf_rows = wf.rearrange("(q t i) n -> t q i n", t=PACK, i=8)
         for t in range(PACK):
             nc.sync.dma_start(wf_raw[:, t * N : (t + 1) * N], wf_rows[t])
+
+        def run_pass(x, a, half):
+            for blk in range(BANKS):
+                multiply(x, a, half, blk)
+                if a == PASSES - 1:
+                    empty(x, half, blk)
+
         for half in range(2):
             gather(0, 0, half)
-            for blk in range(BANKS):
-                multiply(0, 0, half, blk)
-        gather(1, 0, 0)
+            run_pass(0, 0, half)
+        gather(2, 0, 0)
         quantise_wc(0)
         for half in range(2):
             gather(0, 1, half)
-            for blk in range(BANKS):
-                multiply(0, 1, half, blk)
-                empty(0, half, blk)
-        round_wc(1, wc_raw)
+            run_pass(0, 1, half)
+        quantise_wc(1)
+        gather(2, 1, 0)
+        project(2, 0)
+        gather(1, 0, 0)
         deal(wb_codes[:], wb_raw[:], 8)
         gather(1, 1, 0)
         project(1, 0)
-        for a in range(PASSES):
-            gather(1, a, 1)
-        project(1, 1)
-        quantise_wc(1)
-        for a in range(PASSES):
-            gather(2, a, 0)
-        wf_bf = kept("wf_bf", PACK * N, BF16)
+        wf_bf = kept("wf_bf", PACK * N, BF16, tag="g110")
         nc.scalar.copy(
             wf_bf[:].rearrange("p (t m j) -> p m j t", t=PACK, j=PACK),
             wf_raw[:].rearrange("p (j m t) -> p m j t", t=PACK, j=PACK),
         )
-        project(2, 0)
-        for a in range(PASSES):
-            gather(2, a, 1)
-        project(2, 1)
+        for x in (2, 1):
+            for a in range(PASSES):
+                gather(x, a, 1)
+            project(x, 1)
 
         highs = [kept(f"high{half}", PACK * HALF, BF16) for half in range(2)]
         lows = [kept(f"low{half}", PACK * HALF, BF16) for half in range(2)]
@@ -243,13 +244,13 @@ def tile_list_triplex_median_fault_kernel(
             nc.vector.tensor_tensor(part(out, j0, width), part(in0, j0, width), part(in1, j0, width), op)
 
         def high(j0, width):
-            pick(highs, sums[0], sums[1], MAX, j0, width)
+            pick(highs, sums[0], sums[2], MAX, j0, width)
 
         def low(j0, width):
-            pick(lows, sums[0], sums[1], MIN, j0, width)
+            pick(lows, sums[0], sums[2], MIN, j0, width)
 
         def clip(j0, width):
-            pick(clips, highs, sums[2], MIN, j0, width)
+            pick(clips, highs, sums[1], MIN, j0, width)
 
         def median(j0, width):
             pick(medians, lows, clips, MAX, j0, width)

@@ -55,13 +55,13 @@ def tile_list_triplex_median_fault_kernel(
         first_scales = kept("first_scales", PASSES * FIRST, U8)
         bias = kept("bias", PACK, F32)
         a_rows = kept("a_rows", S, U8)
-        bc_rows = kept("bc_rows", 2 * S, U8)
+        bc_rows = kept("bc_rows", 2 * S, U8, tag="late_rows")
 
         def load_scale_rows(eng, dst, src):
             eng.dma_start(dst[0:ROWS, :].bitcast(I32), src.rearrange("a q t -> q a t").bitcast(I32))
 
         def place_scale_rows(dst, src):
-            for q in range(QUADS):
+            for q in (0, 2, 1, 3):
                 nc.scalar.dma_start(
                     dst[32 * q : 32 * q + 4, :].bitcast(I32).rearrange("r (a w) -> r a w", a=PASSES),
                     src[8 * q : 8 * q + 8, :].bitcast(I32),
@@ -187,7 +187,7 @@ def tile_list_triplex_median_fault_kernel(
                     multiply(x, a, half, blk)
                 empty(x, half, blk)
 
-        wf_raw = kept("wf_raw", PACK * N, F32, tag="wc_raw0")
+        wf_raw = kept("wf_raw", PACK * N, F32, tag="late_rows")
         wf_rows = wf.rearrange("(q t i) n -> t q i n", t=PACK, i=8)
         for t in range(PACK):
             nc.sync.dma_start(wf_raw[:, t * N : (t + 1) * N], wf_rows[t])

@@ -157,29 +157,33 @@ def tile_list_triplex_median_fault_kernel(
         banks = {}
 
         def multiply(x, a, half, blk):
+            slices = range(PACK) if x == 0 else range(2 * (blk % 2), 2 * (blk % 2) + 2)
+            width = HALF // len(slices)
             if a == 0:
-                banks[x, half, blk] = psum.tile([P, PACK, BLOCK], F32, name=f"bank{(half, 1, 0)[x] * BANKS + blk}")
+                banks[x, half, blk] = psum.tile(
+                    [P, len(slices), width], F32, name=f"bank{(half, 1, 0)[x] * BANKS + blk}"
+                )
             bank = banks[x, half, blk]
-            j0 = blk * BLOCK
+            j0 = blk * BLOCK // width * width
             s0 = half * HALF + j0 + (a * FIRST + 2 * H if x == 0 else (2 * a + x - 1) * S)
             plane = first_scales if x == 0 else bc_scales
-            for t in range(PACK):
+            for e, t in enumerate(slices):
                 codes, scales = stationary(x, a, t)
                 nc.tensor.matmul_mx(
-                    out=bank[:, t, :], lhsT=codes, lhsT_scale=scales,
-                    rhs=words[x, a, half][:, j0 : j0 + BLOCK].bitcast(FP8X4),
-                    rhs_scale=plane[:, s0 : s0 + BLOCK],
-                    start=(a == 0 and t == 0), stop=(a == PASSES - 1 and t == PACK - 1),
+                    out=bank[:, e, :], lhsT=codes, lhsT_scale=scales,
+                    rhs=words[x, a, half][:, j0 : j0 + width].bitcast(FP8X4),
+                    rhs_scale=plane[:, s0 : s0 + width],
+                    start=(a == 0 and e == 0), stop=(a == PASSES - 1 and e == len(slices) - 1),
                 )
 
         def empty(x, half, blk):
-            j0 = blk * BLOCK
-            dst = sums[x][half][:, PACK * j0 : PACK * (j0 + BLOCK)].rearrange("p (c i t) -> p c t i", t=PACK, i=4)
-            src = banks[x, half, blk][:].rearrange("p t (c i) -> p c t i", i=4)
+            dst = sums[x][half][:].rearrange("p (c u j e) -> p c u j e", c=2, u=2, e=2)[:, blk // 2]
             if x == 0:
-                nc.scalar.activation(dst, src, IDENTITY)
+                j0 = blk % 2 * BLOCK
+                src = banks[x, half, blk][:].rearrange("p (u e) j -> p u j e", u=2)
+                nc.scalar.activation(dst[:, :, j0 : j0 + BLOCK, :], src, IDENTITY)
             else:
-                nc.scalar.copy(dst, src)
+                nc.scalar.copy(dst[:, blk % 2], banks[x, half, blk][:].rearrange("p e j -> p j e"))
 
         def project(x, half):
             for blk in range(BANKS):
@@ -253,7 +257,12 @@ def tile_list_triplex_median_fault_kernel(
             pick(clips, highs, sums[1], MIN, j0, width)
 
         def median(j0, width):
-            pick(medians, lows, clips, MAX, j0, width)
+            nc.vector.tensor_tensor(
+                part(medians, j0, width).rearrange("p (j u e) -> p j u e", u=2, e=2),
+                part(lows, j0, width).rearrange("p (u j e) -> p j u e", u=2, e=2),
+                part(clips, j0, width).rearrange("p (u j e) -> p j u e", u=2, e=2),
+                MAX,
+            )
 
         def score(c):
             j0, width = CHUNKS[c]

@@ -21,13 +21,20 @@ P = 128
 PACK = 4
 PASSES = K // (P * PACK)
 HALF = S // 2
+QUARTER = S // 4
 BLOCK = 128
 BANKS = HALF // BLOCK
-CHUNKS = ((0, 256), (256, 256), (512, 256), (768, 128), (896, 128))
 QUADS = 4
 ROWS = 32
 FIRST = 2 * H + S
-SCALAR_WEAVES = ()
+A, B, C = 0, 1, 2
+
+WF_AT = 0
+TABLE1_AT = WF_AT + 4 * PACK * N
+WA_AT = TABLE1_AT - H * PASSES
+WB_AT = TABLE1_AT + 4 * T
+BIAS_AT = WB_AT + 4 * PASSES * H
+FIRST_AT = BIAS_AT - FIRST // 2
 
 
 def tile_list_triplex_median_fault_kernel(
@@ -37,25 +44,18 @@ def tile_list_triplex_median_fault_kernel(
     nc = tc.nc
     with ExitStack() as ctx:
         keep = ctx.enter_context(tc.tile_pool(name="keep", bufs=1))
-        late = ctx.enter_context(tc.tile_pool(name="late", bufs=1))
+        shared = ctx.enter_context(tc.tile_pool(name="shared", bufs=1))
         psum = ctx.enter_context(tc.psum_pool(name="psum", bufs=1))
 
-        def kept(name, width, dtype, tag=None):
-            return keep.tile([P, width], dtype, name=name, tag=tag or name, align_bytes=64)
+        def kept(name, width, dtype):
+            return keep.tile([P, width], dtype, name=name, align_bytes=64)
 
         def placed(name, width, dtype, offset):
-            return late.tile([P, width], dtype, name=name, offset=offset, align_bytes=64)
+            return shared.tile([P, width], dtype, name=name, offset=offset, align_bytes=64)
 
         lists = [keep.tile([P, S // 16], U16, name=f"list{x}") for x in range(3)]
         scale_win = kept("scale_win", T, U8)
-        word_win = [kept(f"word_win{a}", T, I32) for a in range(PASSES)]
-        wa_raw = kept("wa_raw", PASSES * 2 * H, U8)[:]
         ws_raw = kept("ws_raw", 2 * H, U8)
-        first_rows = kept("first_rows", FIRST, U8)
-        first_scales = kept("first_scales", PASSES * FIRST, U8)
-        bias = kept("bias", PACK, F32)
-        a_rows = kept("a_rows", S, U8)
-        bc_rows = kept("bc_rows", 2 * S, U8, tag="late_rows")
 
         def load_scale_rows(eng, dst, src):
             eng.dma_start(dst[0:ROWS, :].bitcast(I32), src.rearrange("a q t -> q a t").bitcast(I32))
@@ -67,13 +67,8 @@ def tile_list_triplex_median_fault_kernel(
                     src[8 * q : 8 * q + 8, :].bitcast(I32),
                 )
 
-        def load_words(a):
-            nc.sync.dma_start(word_win[a][:], tab_words[a].rearrange("p t i -> p (t i)").bitcast(I32))
-
-        def load_wc(a):
-            raw = kept(f"wc_raw{a}", PACK * H, F32)
-            nc.sync.dma_start(raw[:], wc[512 * a : 512 * (a + 1), :].rearrange("(p j) r -> p (j r)", j=PACK))
-            return raw
+        def load_words(win, a):
+            nc.sync.dma_start(win[:], tab_words[a].rearrange("p t i -> p (t i)").bitcast(I32))
 
         def deal(dst, src, run):
             nc.vector.tensor_copy(
@@ -81,75 +76,91 @@ def tile_list_triplex_median_fault_kernel(
                 src.rearrange("p (a q t w) -> p a t q w", a=2, t=PACK, w=run),
             )
 
-        wc_bf = [kept("wc_bf0", PACK * H, BF16), placed("wc_bf1", PACK * H, BF16, 4096)]
-
-        def round_wc(a):
-            dst = wc_bf[a][:].rearrange("p (t q u i j) -> p u q t j i", t=PACK, u=2, i=4, j=PACK)
-            src = wc_raw[a][:].rearrange("p (j q t u i) -> p u q t j i", t=PACK, u=2, i=4, j=PACK)
-            for u in range(2):
-                nc.scalar.copy(dst[:, u], src[:, u])
-
-        nc.sync.dma_start(lists[0][:], offs)
+        nc.sync.dma_start(lists[A][:], offs)
         load_scale_rows(nc.sync, scale_win[:], tab_scales)
         load_scale_rows(nc.scalar, ws_raw[:, 0:H], wa_scales)
         load_scale_rows(nc.scalar, ws_raw[:, H : 2 * H], wb_scales)
-        nc.sync.dma_start(lists[1][:], offs2)
-        nc.sync.dma_start(lists[2][:], offs3)
+        nc.sync.dma_start(lists[B][:], offs2)
+        nc.sync.dma_start(lists[C][:], offs3)
+        wa_raw = placed("wa_raw", PASSES * 2 * H, U8, WA_AT)
         nc.sync.dma_start(
-            wa_raw.bitcast(I32).rearrange("p (a w) -> p a w", a=PASSES),
+            wa_raw[:].bitcast(I32).rearrange("p (a w) -> p a w", a=PASSES),
             wa_words.bitcast(I32).rearrange("a p w -> p a w"),
         )
-        load_words(0)
-        wc_raw = [load_wc(a) for a in range(PASSES)]
-        load_words(1)
-        wb_raw = placed("wb_raw", PASSES * H, I32, 0)
-        nc.sync.dma_start(
-            wb_raw[:].rearrange("p (a w) -> p a w", a=PASSES),
-            wb_words.rearrange("a p e i -> a p (e i)").bitcast(I32).rearrange("a p w -> p a w"),
-        )
-        nc.sync.dma_start(bias[:], bf.rearrange("(p t) -> p t", t=PACK))
+        word_win = [kept("word_win0", T, I32)]
+        load_words(word_win[0], 0)
+        wc_raw = [kept(f"wc_raw{a}", PACK * H, F32) for a in range(PASSES)]
+        for a in range(PASSES):
+            nc.sync.dma_start(wc_raw[a][:], wc[512 * a : 512 * (a + 1), :].rearrange("(p j) r -> p (j r)", j=PACK))
 
         nc.vector.memset(scale_win[32:64, :].bitcast(I32), 0)
         nc.vector.memset(scale_win[64:P, :].bitcast(I32), 0)
 
-        nc.vector.tensor_copy(a_rows[:], scale_win[:].indirect(lists[0][:]))
+        a_rows = kept("a_rows", S, U8)
+        first_rows = placed("first_rows", FIRST, U8, FIRST_AT)
+        first_scales = kept("first_scales", PASSES * FIRST, U8)
+        nc.vector.tensor_copy(a_rows[:], scale_win[:].indirect(lists[A][:]))
         deal(first_rows[0:ROWS, 0 : 2 * H].bitcast(I32), ws_raw[0:ROWS, :].bitcast(I32), 2)
         nc.vector.tensor_copy(first_rows[0:ROWS, 2 * H : FIRST].bitcast(I32), a_rows[0:ROWS, :].bitcast(I32))
         place_scale_rows(first_scales[:], first_rows[:])
         wa_codes = kept("wa_codes", PASSES * 2 * H, U8)
-        deal(wa_codes[:].bitcast(I32), wa_raw.bitcast(I32), 4)
-        for x in range(1, 3):
+        deal(wa_codes[:].bitcast(I32), wa_raw[:].bitcast(I32), 4)
+
+        wf_raw = placed("wf_raw", PACK * N, F32, WF_AT)
+        wf_rows = wf.rearrange("(q t i) n -> t q i n", t=PACK, i=8)
+        for t in range(PACK):
+            nc.sync.dma_start(wf_raw[:, t * N : (t + 1) * N], wf_rows[t])
+        word_win.append(placed("word_win1", T, I32, TABLE1_AT))
+        load_words(word_win[1], 1)
+        wb_raw = placed("wb_raw", PASSES * H, I32, WB_AT)
+        nc.sync.dma_start(
+            wb_raw[:].rearrange("p (a w) -> p a w", a=PASSES),
+            wb_words.rearrange("a p e i -> a p (e i)").bitcast(I32).rearrange("a p w -> p a w"),
+        )
+        bias = placed("bias", PACK, F32, BIAS_AT)
+        nc.sync.dma_start(bias[:], bf.rearrange("(p t) -> p t", t=PACK))
+
+        bc_rows = kept("bc_rows", 2 * S, U8)
+        for x in (C, B):
             nc.vector.tensor_copy(bc_rows[:, (x - 1) * S : x * S], scale_win[:].indirect(lists[x][:]))
+
+        wc_bf = [kept(f"wc_bf{a}", PACK * H, BF16) for a in range(PASSES)]
         for a in range(PASSES):
-            round_wc(a)
-        bc_scales = kept("bc_scales", PASSES * 2 * S, U8, tag="wc_raw1")
+            dst = wc_bf[a][:].rearrange("p (t q u i j) -> p u q t j i", t=PACK, u=2, i=4, j=PACK)
+            src = wc_raw[a][:].rearrange("p (j q t u i) -> p u q t j i", t=PACK, u=2, i=4, j=PACK)
+            for u in range(2):
+                nc.scalar.copy(dst[:, u], src[:, u])
+        wf_bf = kept("wf_bf", PACK * N, BF16)
+        nc.scalar.copy(
+            wf_bf[:].rearrange("p (t m j) -> p m j t", t=PACK, j=PACK),
+            wf_raw[:].rearrange("p (j m t) -> p m j t", t=PACK, j=PACK),
+        )
+        bc_scales = placed("bc_scales", PASSES * 2 * S, U8, WF_AT)
         place_scale_rows(bc_scales[:], bc_rows[:])
 
         words = {}
-        after = {(2, 0, 1): 0, (2, 1, 1): 2048, (1, 0, 0): 4096, (1, 1, 1): 6144}
 
-        def gather(x, a, half):
+        def gather(x, a, half, halves=1, at=None):
             name = "g%d%d%d" % (x, a, half)
-            if (x, a, half) in after:
-                g = placed(name, HALF, U32, after[x, a, half])
-            else:
-                g = kept(name, HALF, U32, tag="g011" if name == "g101" else None)
-            cols = slice(half * HALF // 16, (half + 1) * HALF // 16)
+            width = halves * HALF
+            g = kept(name, width, U32) if at is None else placed(name, width, U32, at)
+            cols = slice(half * HALF // 16, (half * HALF + width) // 16)
             nc.vector.tensor_copy(g[:], word_win[a][:].bitcast(U32).indirect(lists[x][:, cols]))
-            words[x, a, half] = g
+            for e in range(halves):
+                words[x, a, half + e] = g[:, e * HALF : (e + 1) * HALF]
 
         wb_codes = kept("wb_codes", PASSES * H, I32)
         wc_codes = [kept(f"wc_codes{a}", H, U32) for a in range(PASSES)]
         wc_scales = [kept(f"wc_scales{a}", H, U8) for a in range(PASSES)]
-        def quantise_wc(a):
-            nc.vector.quantize_mx(out=wc_codes[a][:].bitcast(FP8X4), scales=wc_scales[a][:], in_=wc_bf[a][:])
+        wf_codes = kept("wf_codes", N, U32)
+        wf_scales = kept("wf_scales", N, U8)
 
         def stationary(x, a, t):
             lo = a * H + t * P
             s0 = a * FIRST + x * H + t * P
-            if x == 0:
+            if x == A:
                 return wa_codes[:, 2 * lo : 2 * (lo + P)].bitcast(FP4X4), first_scales[:, s0 : s0 + P]
-            if x == 1:
+            if x == B:
                 return wb_codes[:, lo : lo + P].bitcast(FP8X4), first_scales[:, s0 : s0 + P]
             return wc_codes[a][:, t * P : (t + 1) * P].bitcast(FP8X4), wc_scales[a][:, t * P : (t + 1) * P]
 
@@ -157,7 +168,7 @@ def tile_list_triplex_median_fault_kernel(
         banks = {}
 
         def multiply(x, a, half, blk):
-            slices = range(PACK) if x == 0 else range(2 * (blk % 2), 2 * (blk % 2) + 2)
+            slices = range(PACK) if x == A else range(2 * (blk % 2), 2 * (blk % 2) + 2)
             width = HALF // len(slices)
             if a == 0:
                 banks[x, half, blk] = psum.tile(
@@ -165,8 +176,8 @@ def tile_list_triplex_median_fault_kernel(
                 )
             bank = banks[x, half, blk]
             j0 = blk * BLOCK // width * width
-            s0 = half * HALF + j0 + (a * FIRST + 2 * H if x == 0 else (2 * a + x - 1) * S)
-            plane = first_scales if x == 0 else bc_scales
+            s0 = half * HALF + j0 + (a * FIRST + 2 * H if x == A else (2 * a + x - 1) * S)
+            plane = first_scales if x == A else bc_scales
             for e, t in enumerate(slices):
                 codes, scales = stationary(x, a, t)
                 nc.tensor.matmul_mx(
@@ -178,7 +189,7 @@ def tile_list_triplex_median_fault_kernel(
 
         def empty(x, half, blk):
             dst = sums[x][half][:].rearrange("p (c u j e) -> p c u j e", c=2, u=2, e=2)[:, blk // 2]
-            if x == 0:
+            if x == A:
                 j0 = blk % 2 * BLOCK
                 src = banks[x, half, blk][:].rearrange("p (u e) j -> p u j e", u=2)
                 nc.scalar.activation(dst[:, :, j0 : j0 + BLOCK, :], src, IDENTITY)
@@ -191,54 +202,46 @@ def tile_list_triplex_median_fault_kernel(
                     multiply(x, a, half, blk)
                 empty(x, half, blk)
 
-        wf_raw = kept("wf_raw", PACK * N, F32, tag="late_rows")
-        wf_rows = wf.rearrange("(q t i) n -> t q i n", t=PACK, i=8)
-        for t in range(PACK):
-            nc.sync.dma_start(wf_raw[:, t * N : (t + 1) * N], wf_rows[t])
-
         def run_pass(x, a, half):
             for blk in range(BANKS):
                 multiply(x, a, half, blk)
                 if a == PASSES - 1:
                     empty(x, half, blk)
 
+        gather(A, 0, 0, halves=2)
         for half in range(2):
-            gather(0, 0, half)
-            run_pass(0, 0, half)
-        gather(2, 0, 0)
-        quantise_wc(0)
+            run_pass(A, 0, half)
+        gather(C, 0, 0, halves=2)
+        gather(B, 0, 0)
+        for a in range(PASSES):
+            nc.vector.quantize_mx(out=wc_codes[a][:].bitcast(FP8X4), scales=wc_scales[a][:], in_=wc_bf[a][:])
+        nc.vector.quantize_mx(out=wf_codes[:].bitcast(FP8X4), scales=wf_scales[:], in_=wf_bf[:])
         for half in range(2):
-            gather(0, 1, half)
-            run_pass(0, 1, half)
-        quantise_wc(1)
-        gather(2, 1, 0)
-        project(2, 0)
-        gather(1, 0, 0)
+            gather(A, 1, half)
+            run_pass(A, 1, half)
+        gather(C, 1, 0)
+        project(C, 0)
         deal(wb_codes[:], wb_raw[:], 8)
-        gather(1, 1, 0)
-        project(1, 0)
-        wf_bf = kept("wf_bf", PACK * N, BF16, tag="g110")
-        nc.scalar.copy(
-            wf_bf[:].rearrange("p (t m j) -> p m j t", t=PACK, j=PACK),
-            wf_raw[:].rearrange("p (j m t) -> p m j t", t=PACK, j=PACK),
-        )
-        for x in (2, 1):
-            for a in range(PASSES):
-                gather(x, a, 1)
-            project(x, 1)
+        gather(B, 1, 0)
+        project(B, 0)
+        gather(C, 1, 1)
+        project(C, 1)
+        gather(B, 0, 1, at=WB_AT)
+        gather(B, 1, 1)
+        project(B, 1)
 
         highs = [kept(f"high{half}", PACK * HALF, BF16) for half in range(2)]
         lows = [kept(f"low{half}", PACK * HALF, BF16) for half in range(2)]
         clips = [kept(f"clip{half}", PACK * HALF, BF16) for half in range(2)]
         medians = [kept(f"median{half}", PACK * HALF, BF16) for half in range(2)]
-        wf_codes = kept("wf_codes", N, U32)
-        wf_scales = kept("wf_scales", N, U8)
         y_bf = [kept(f"y_bf{half}", PACK * HALF, BF16) for half in range(2)]
         y_codes = [kept(f"y_codes{half}", HALF, U32) for half in range(2)]
         y_scales = kept("y_scales", S, U8)
+        h_codes = kept("h_codes", S, U32)
+        h_scales = kept("h_scales", S, U8)
         y_rows = out_0.rearrange("(p t) j -> p t j", t=PACK)
         y_words = out_1[0].rearrange("p m i -> p (m i)").bitcast(I32)
-        state = {}
+        scores = {}
 
         def part(tiles, j0, width):
             half, off = divmod(j0, HALF)
@@ -247,51 +250,55 @@ def tile_list_triplex_median_fault_kernel(
         def pick(out, in0, in1, op, j0, width):
             nc.vector.tensor_tensor(part(out, j0, width), part(in0, j0, width), part(in1, j0, width), op)
 
-        def high(j0, width):
-            pick(highs, sums[0], sums[2], MAX, j0, width)
+        def bounds(half):
+            pick(highs, sums[A], sums[C], MAX, half * HALF, HALF)
+            pick(lows, sums[A], sums[C], MIN, half * HALF, HALF)
 
-        def low(j0, width):
-            pick(lows, sums[0], sums[2], MIN, j0, width)
-
-        def clip(j0, width):
-            pick(clips, highs, sums[1], MIN, j0, width)
+        def clip(j0):
+            pick(clips, highs, sums[B], MIN, j0, QUARTER)
 
         def median(j0, width):
+            q0 = j0 // QUARTER * QUARTER
+            cols = slice(j0 - q0, j0 - q0 + width)
             nc.vector.tensor_tensor(
                 part(medians, j0, width).rearrange("p (j u e) -> p j u e", u=2, e=2),
-                part(lows, j0, width).rearrange("p (u j e) -> p j u e", u=2, e=2),
-                part(clips, j0, width).rearrange("p (u j e) -> p j u e", u=2, e=2),
+                part(lows, q0, QUARTER).rearrange("p (u j e) -> p j u e", u=2, e=2)[:, cols],
+                part(clips, q0, QUARTER).rearrange("p (u j e) -> p j u e", u=2, e=2)[:, cols],
                 MAX,
             )
 
-        def score(c):
-            j0, width = CHUNKS[c]
-            h_codes = kept(f"h_codes{c}", width, U32)
-            h_scales = kept(f"h_scales{c}", width, U8)
-            nc.vector.quantize_mx(out=h_codes[:].bitcast(FP8X4), scales=h_scales[:], in_=part(medians, j0, width))
-            y = kept(f"y{c}", PACK * width, F32)
-            for pair in range(2):
-                bank = psum.tile([P, 2, width], F32, name=f"bank{2 * (c % 2) + pair}")
-                for u in range(2):
-                    t = 2 * pair + u
+        def quantise_h(j0, width):
+            nc.vector.quantize_mx(
+                out=h_codes[:, j0 : j0 + width].bitcast(FP8X4), scales=h_scales[:, j0 : j0 + width],
+                in_=part(medians, j0, width),
+            )
+
+        def score(j0, width, first_bank):
+            y = kept(f"y{j0}", PACK * width, F32)
+            per_bank = 1 if width == HALF else 2
+            for n in range(PACK // per_bank):
+                bank = psum.tile([P, per_bank, width], F32, name=f"bank{first_bank + n}")
+                for u in range(per_bank):
+                    t = per_bank * n + u
                     nc.tensor.matmul_mx(
                         out=bank[:, u, :], lhsT=wf_codes[:, t * P : (t + 1) * P].bitcast(FP8X4),
                         lhsT_scale=wf_scales[:, t * P : (t + 1) * P],
-                        rhs=h_codes[:].bitcast(FP8X4), rhs_scale=h_scales[:], start=True, stop=True,
+                        rhs=h_codes[:, j0 : j0 + width].bitcast(FP8X4), rhs_scale=h_scales[:, j0 : j0 + width],
+                        start=True, stop=True,
                     )
-                for u in range(2):
-                    t = 2 * pair + u
+                for u in range(per_bank):
+                    t = per_bank * n + u
                     nc.scalar.activation(
                         y[:, t * width : (t + 1) * width], bank[:, u, :], IDENTITY, bias=bias[:, t : t + 1]
                     )
             nc.sync.dma_start(y_rows[:, :, j0 : j0 + width], y[:].rearrange("p (t j) -> p t j", t=PACK))
-            state["y", c] = y
+            for j in range(j0, j0 + width, BLOCK):
+                scores[j] = y[:].rearrange("p (t j) -> p t j", t=PACK)[:, :, j - j0 :]
 
-        def weave(c):
-            copy = nc.scalar.copy if c in SCALAR_WEAVES else nc.vector.tensor_copy
+        def weave(copy, j0, width):
             copy(
-                part(y_bf, *CHUNKS[c]).rearrange("p (c i t) -> p c t i", t=PACK, i=4),
-                state["y", c][:].rearrange("p (t c i) -> p c t i", t=PACK, i=4),
+                part(y_bf, j0, width).rearrange("p (c i t) -> p c t i", t=PACK, i=4),
+                scores[j0][:, :, 0:width].rearrange("p t (c i) -> p c t i", i=4),
             )
 
         def planes(j0, width):
@@ -303,35 +310,34 @@ def tile_list_triplex_median_fault_kernel(
             if off + width == HALF:
                 nc.sync.dma_start(y_words[:, half * HALF : (half + 1) * HALF], y_codes[half][:].bitcast(I32))
 
-        high(0, HALF)
-        low(0, HALF)
-        nc.vector.quantize_mx(out=wf_codes[:].bitcast(FP8X4), scales=wf_scales[:], in_=wf_bf[:])
-        for step in (clip, median):
-            step(*CHUNKS[0])
-            step(*CHUNKS[1])
-        score(0)
-        score(1)
-        weave(0)
-        weave(1)
-        third, fourth = (512, 256), (768, 256)
-        high(*third)
-        low(*third)
-        clip(*third)
-        high(*fourth)
-        median(*third)
-        low(*fourth)
-        score(2)
-        clip(*fourth)
-        planes(*CHUNKS[0])
-        median(*fourth)
-        planes(*CHUNKS[1])
-        score(3)
-        score(4)
-        weave(2)
-        weave(3)
-        planes(*third)
-        weave(4)
-        planes(*fourth)
+        bounds(0)
+        clip(0)
+        clip(256)
+        median(0, 256)
+        median(256, 256)
+        quantise_h(0, 256)
+        quantise_h(256, 256)
+        score(0, HALF, 0)
+        bounds(1)
+        clip(512)
+        clip(768)
+        median(512, 256)
+        median(768, 128)
+        quantise_h(512, 256)
+        median(896, 128)
+        quantise_h(768, 128)
+        weave(nc.scalar.copy, 0, 256)
+        score(512, 256, 4)
+        weave(nc.vector.tensor_copy, 256, 256)
+        quantise_h(896, 128)
+        score(768, 128, 6)
+        score(896, 128, 0)
+        planes(0, HALF)
+        weave(nc.vector.tensor_copy, 512, 256)
+        weave(nc.vector.tensor_copy, 768, 128)
+        planes(512, 256)
+        weave(nc.vector.tensor_copy, 896, 128)
+        planes(768, 256)
         for q in range(QUADS):
             eng = nc.scalar if q % 2 else nc.sync
             eng.dma_start(out_2[0, 4 * q : 4 * q + 4, :].bitcast(I32), y_scales[32 * q : 32 * q + 4, :].bitcast(I32))

@@ -29,12 +29,13 @@ ROWS = 32
 FIRST = 2 * H + S
 A, B, C = 0, 1, 2
 
-WF_AT = 0
-TABLE1_AT = WF_AT + 4 * PACK * N
-WA_AT = TABLE1_AT - H * PASSES
+TABLE1_AT = 0
+WA_AT = TABLE1_AT
 WB_AT = TABLE1_AT + 4 * T
 BIAS_AT = WB_AT + 4 * PASSES * H
+WF_AT = BIAS_AT + 64
 FIRST_AT = BIAS_AT - FIRST // 2
+LAST_C_AT = WF_AT + 4 * PACK * N
 
 
 def tile_list_triplex_median_fault_kernel(
@@ -60,9 +61,9 @@ def tile_list_triplex_median_fault_kernel(
         def load_scale_rows(eng, dst, src):
             eng.dma_start(dst[0:ROWS, :].bitcast(I32), src.rearrange("a q t -> q a t").bitcast(I32))
 
-        def place_scale_rows(dst, src):
+        def place_scale_rows(eng, dst, src):
             for q in (0, 2, 1, 3):
-                nc.scalar.dma_start(
+                eng.dma_start(
                     dst[32 * q : 32 * q + 4, :].bitcast(I32).rearrange("r (a w) -> r a w", a=PASSES),
                     src[8 * q : 8 * q + 8, :].bitcast(I32),
                 )
@@ -102,16 +103,17 @@ def tile_list_triplex_median_fault_kernel(
         nc.vector.tensor_copy(a_rows[:], scale_win[:].indirect(lists[A][:]))
         deal(first_rows[0:ROWS, 0 : 2 * H].bitcast(I32), ws_raw[0:ROWS, :].bitcast(I32), 2)
         nc.vector.tensor_copy(first_rows[0:ROWS, 2 * H : FIRST].bitcast(I32), a_rows[0:ROWS, :].bitcast(I32))
-        place_scale_rows(first_scales[:], first_rows[:])
+        place_scale_rows(nc.scalar, first_scales[:], first_rows[:])
         wa_codes = kept("wa_codes", PASSES * 2 * H, U8)
         deal(wa_codes[:].bitcast(I32), wa_raw[:].bitcast(I32), 4)
 
-        wf_raw = placed("wf_raw", PACK * N, F32, WF_AT)
-        wf_rows = wf.rearrange("(q t i) n -> t q i n", t=PACK, i=8)
-        for t in range(PACK):
-            nc.sync.dma_start(wf_raw[:, t * N : (t + 1) * N], wf_rows[t])
         word_win.append(placed("word_win1", T, I32, TABLE1_AT))
         load_words(word_win[1], 1)
+        bc_rows = kept("bc_rows", 2 * S, U8)
+        for x in (C, B):
+            nc.vector.tensor_copy(bc_rows[:, (x - 1) * S : x * S], scale_win[:].indirect(lists[x][:]))
+        bc_scales = kept("bc_scales", PASSES * 2 * S, U8)
+        place_scale_rows(nc.sync, bc_scales[:], bc_rows[:])
         wb_raw = placed("wb_raw", PASSES * H, I32, WB_AT)
         nc.sync.dma_start(
             wb_raw[:].rearrange("p (a w) -> p a w", a=PASSES),
@@ -119,10 +121,10 @@ def tile_list_triplex_median_fault_kernel(
         )
         bias = placed("bias", PACK, F32, BIAS_AT)
         nc.sync.dma_start(bias[:], bf.rearrange("(p t) -> p t", t=PACK))
-
-        bc_rows = kept("bc_rows", 2 * S, U8)
-        for x in (C, B):
-            nc.vector.tensor_copy(bc_rows[:, (x - 1) * S : x * S], scale_win[:].indirect(lists[x][:]))
+        wf_raw = placed("wf_raw", PACK * N, F32, WF_AT)
+        wf_rows = wf.rearrange("(q t i) n -> t q i n", t=PACK, i=8)
+        for t in range(PACK):
+            nc.sync.dma_start(wf_raw[:, t * N : (t + 1) * N], wf_rows[t])
 
         wc_bf = [kept(f"wc_bf{a}", PACK * H, BF16) for a in range(PASSES)]
         for a in range(PASSES):
@@ -130,13 +132,6 @@ def tile_list_triplex_median_fault_kernel(
             src = wc_raw[a][:].rearrange("p (j q t u i) -> p u q t j i", t=PACK, u=2, i=4, j=PACK)
             for u in range(2):
                 nc.scalar.copy(dst[:, u], src[:, u])
-        wf_bf = kept("wf_bf", PACK * N, BF16)
-        nc.scalar.copy(
-            wf_bf[:].rearrange("p (t m j) -> p m j t", t=PACK, j=PACK),
-            wf_raw[:].rearrange("p (j m t) -> p m j t", t=PACK, j=PACK),
-        )
-        bc_scales = placed("bc_scales", PASSES * 2 * S, U8, WF_AT)
-        place_scale_rows(bc_scales[:], bc_rows[:])
 
         words = {}
 
@@ -164,7 +159,7 @@ def tile_list_triplex_median_fault_kernel(
                 return wb_codes[:, lo : lo + P].bitcast(FP8X4), first_scales[:, s0 : s0 + P]
             return wc_codes[a][:, t * P : (t + 1) * P].bitcast(FP8X4), wc_scales[a][:, t * P : (t + 1) * P]
 
-        sums = [[kept(f"sum{x}_{half}", PACK * HALF, BF16) for half in range(2)] for x in range(3)]
+        sums = [[kept(f"sum{x}_{half}", PACK * HALF, BF16) for half in range(2 - (x == B))] for x in range(3)]
         banks = {}
 
         def multiply(x, a, half, blk):
@@ -172,7 +167,7 @@ def tile_list_triplex_median_fault_kernel(
             width = HALF // len(slices)
             if a == 0:
                 banks[x, half, blk] = psum.tile(
-                    [P, len(slices), width], F32, name=f"bank{(half, 1, 0)[x] * BANKS + blk}"
+                    [P, len(slices), width], F32, name=f"bank{(half + (x == C)) % 2 * BANKS + blk}"
                 )
             bank = banks[x, half, blk]
             j0 = blk * BLOCK // width * width
@@ -196,11 +191,12 @@ def tile_list_triplex_median_fault_kernel(
             else:
                 nc.scalar.copy(dst[:, blk % 2], banks[x, half, blk][:].rearrange("p e j -> p j e"))
 
-        def project(x, half):
+        def project(x, half, emptied=True):
             for blk in range(BANKS):
                 for a in range(PASSES):
                     multiply(x, a, half, blk)
-                empty(x, half, blk)
+                if emptied:
+                    empty(x, half, blk)
 
         def run_pass(x, a, half):
             for blk in range(BANKS):
@@ -208,27 +204,33 @@ def tile_list_triplex_median_fault_kernel(
                 if a == PASSES - 1:
                     empty(x, half, blk)
 
-        gather(A, 0, 0, halves=2)
-        for half in range(2):
-            run_pass(A, 0, half)
-        gather(C, 0, 0, halves=2)
+        gather(A, 0, 0)
+        run_pass(A, 0, 0)
+        gather(C, 0, 0)
         gather(B, 0, 0)
+        gather(A, 0, 1)
+        gather(C, 0, 1)
         for a in range(PASSES):
             nc.vector.quantize_mx(out=wc_codes[a][:].bitcast(FP8X4), scales=wc_scales[a][:], in_=wc_bf[a][:])
-        nc.vector.quantize_mx(out=wf_codes[:].bitcast(FP8X4), scales=wf_scales[:], in_=wf_bf[:])
-        for half in range(2):
-            gather(A, 1, half)
-            run_pass(A, 1, half)
+        gather(A, 1, 0)
+        run_pass(A, 1, 0)
         gather(C, 1, 0)
         project(C, 0)
-        deal(wb_codes[:], wb_raw[:], 8)
         gather(B, 1, 0)
+        deal(wb_codes[:], wb_raw[:], 8)
         project(B, 0)
-        gather(C, 1, 1)
+        gather(A, 1, 1)
+        project(A, 1)
+        gather(C, 1, 1, at=LAST_C_AT)
         project(C, 1)
         gather(B, 0, 1, at=WB_AT)
         gather(B, 1, 1)
-        project(B, 1)
+        project(B, 1, emptied=False)
+        wf_bf = placed("wf_bf", PACK * N, BF16, LAST_C_AT)
+        nc.scalar.copy(
+            wf_bf[:].rearrange("p (t m j) -> p m j t", t=PACK, j=PACK),
+            wf_raw[:].rearrange("p (j m t) -> p m j t", t=PACK, j=PACK),
+        )
 
         highs = [kept(f"high{half}", PACK * HALF, BF16) for half in range(2)]
         lows = [kept(f"low{half}", PACK * HALF, BF16) for half in range(2)]
@@ -250,9 +252,18 @@ def tile_list_triplex_median_fault_kernel(
         def pick(out, in0, in1, op, j0, width):
             nc.vector.tensor_tensor(part(out, j0, width), part(in0, j0, width), part(in1, j0, width), op)
 
-        def bounds(half):
-            pick(highs, sums[A], sums[C], MAX, half * HALF, HALF)
-            pick(lows, sums[A], sums[C], MIN, half * HALF, HALF)
+        def bounds(j0, width):
+            pick(highs, sums[A], sums[C], MAX, j0, width)
+            pick(lows, sums[A], sums[C], MIN, j0, width)
+
+        def clip_bank(blk):
+            j0 = HALF + blk // 2 * QUARTER
+            nc.vector.tensor_tensor(
+                part(clips, j0, QUARTER).rearrange("p (u j e) -> p u j e", u=2, e=2)[:, blk % 2],
+                banks[B, 1, blk][:].rearrange("p e j -> p j e"),
+                part(highs, j0, QUARTER).rearrange("p (u j e) -> p u j e", u=2, e=2)[:, blk % 2],
+                MIN,
+            )
 
         def clip(j0):
             pick(clips, highs, sums[B], MIN, j0, QUARTER)
@@ -291,7 +302,10 @@ def tile_list_triplex_median_fault_kernel(
                     nc.scalar.activation(
                         y[:, t * width : (t + 1) * width], bank[:, u, :], IDENTITY, bias=bias[:, t : t + 1]
                     )
-            nc.sync.dma_start(y_rows[:, :, j0 : j0 + width], y[:].rearrange("p (t j) -> p t j", t=PACK))
+                if width == HALF:
+                    nc.sync.dma_start(y_rows[:, n, j0 : j0 + width], y[:, n * width : (n + 1) * width])
+            if width < HALF:
+                nc.sync.dma_start(y_rows[:, :, j0 : j0 + width], y[:].rearrange("p (t j) -> p t j", t=PACK))
             for j in range(j0, j0 + width, BLOCK):
                 scores[j] = y[:].rearrange("p (t j) -> p t j", t=PACK)[:, :, j - j0 :]
 
@@ -310,30 +324,33 @@ def tile_list_triplex_median_fault_kernel(
             if off + width == HALF:
                 nc.sync.dma_start(y_words[:, half * HALF : (half + 1) * HALF], y_codes[half][:].bitcast(I32))
 
-        bounds(0)
+        bounds(0, HALF)
         clip(0)
         clip(256)
         median(0, 256)
         median(256, 256)
         quantise_h(0, 256)
         quantise_h(256, 256)
+        bounds(512, 256)
+        bounds(768, 256)
+        clip_bank(0)
+        clip_bank(1)
+        nc.vector.quantize_mx(out=wf_codes[:].bitcast(FP8X4), scales=wf_scales[:], in_=wf_bf[:])
         score(0, HALF, 0)
-        bounds(1)
-        clip(512)
-        clip(768)
+        clip_bank(2)
+        clip_bank(3)
         median(512, 256)
         median(768, 128)
         quantise_h(512, 256)
         median(896, 128)
         quantise_h(768, 128)
-        weave(nc.scalar.copy, 0, 256)
         score(512, 256, 4)
-        weave(nc.vector.tensor_copy, 256, 256)
         quantise_h(896, 128)
         score(768, 128, 6)
         score(896, 128, 0)
-        planes(0, HALF)
+        weave(nc.vector.tensor_copy, 0, HALF)
         weave(nc.vector.tensor_copy, 512, 256)
+        planes(0, HALF)
         weave(nc.vector.tensor_copy, 768, 128)
         planes(512, 256)
         weave(nc.vector.tensor_copy, 896, 128)

@@ -29,12 +29,8 @@ ROWS = 32
 FIRST = 2 * H + S
 A, B, C = 0, 1, 2
 
-TABLE1_AT = 0
-WA_AT = TABLE1_AT
-WB_AT = TABLE1_AT + 4 * T
-BIAS_AT = WB_AT + 4 * PASSES * H
-WF_AT = BIAS_AT + 64
-FIRST_AT = BIAS_AT - FIRST // 2
+WC1_AT = 0
+WF_AT = WC1_AT + 4 * PACK * H
 LAST_C_AT = WF_AT + 4 * PACK * N
 
 
@@ -83,22 +79,31 @@ def tile_list_triplex_median_fault_kernel(
         load_scale_rows(nc.scalar, ws_raw[:, H : 2 * H], wb_scales)
         nc.sync.dma_start(lists[B][:], offs2)
         nc.sync.dma_start(lists[C][:], offs3)
-        wa_raw = placed("wa_raw", PASSES * 2 * H, U8, WA_AT)
+        wa_raw = kept("wa_raw", PASSES * 2 * H, U8)
         nc.sync.dma_start(
             wa_raw[:].bitcast(I32).rearrange("p (a w) -> p a w", a=PASSES),
             wa_words.bitcast(I32).rearrange("a p w -> p a w"),
         )
         word_win = [kept("word_win0", T, I32)]
         load_words(word_win[0], 0)
-        wc_raw = [kept(f"wc_raw{a}", PACK * H, F32) for a in range(PASSES)]
+        wc_raw = [kept("wc_raw0", PACK * H, F32), placed("wc_raw1", PACK * H, F32, WC1_AT)]
         for a in range(PASSES):
             nc.sync.dma_start(wc_raw[a][:], wc[512 * a : 512 * (a + 1), :].rearrange("(p j) r -> p (j r)", j=PACK))
+        word_win.append(kept("word_win1", T, I32))
+        load_words(word_win[1], 1)
+        wb_raw = kept("wb_raw", PASSES * H, I32)
+        nc.sync.dma_start(
+            wb_raw[:].rearrange("p (a w) -> p a w", a=PASSES),
+            wb_words.rearrange("a p e i -> a p (e i)").bitcast(I32).rearrange("a p w -> p a w"),
+        )
+        bias = kept("bias", PACK, F32)
+        nc.sync.dma_start(bias[:], bf.rearrange("(p t) -> p t", t=PACK))
 
         nc.vector.memset(scale_win[32:64, :].bitcast(I32), 0)
         nc.vector.memset(scale_win[64:P, :].bitcast(I32), 0)
 
         a_rows = kept("a_rows", S, U8)
-        first_rows = placed("first_rows", FIRST, U8, FIRST_AT)
+        first_rows = kept("first_rows", FIRST, U8)
         first_scales = kept("first_scales", PASSES * FIRST, U8)
         nc.vector.tensor_copy(a_rows[:], scale_win[:].indirect(lists[A][:]))
         deal(first_rows[0:ROWS, 0 : 2 * H].bitcast(I32), ws_raw[0:ROWS, :].bitcast(I32), 2)
@@ -107,24 +112,9 @@ def tile_list_triplex_median_fault_kernel(
         wa_codes = kept("wa_codes", PASSES * 2 * H, U8)
         deal(wa_codes[:].bitcast(I32), wa_raw[:].bitcast(I32), 4)
 
-        word_win.append(placed("word_win1", T, I32, TABLE1_AT))
-        load_words(word_win[1], 1)
-        bc_rows = kept("bc_rows", 2 * S, U8)
+        bc_rows = placed("bc_rows", 2 * S, U8, WF_AT)
         for x in (C, B):
             nc.vector.tensor_copy(bc_rows[:, (x - 1) * S : x * S], scale_win[:].indirect(lists[x][:]))
-        bc_scales = kept("bc_scales", PASSES * 2 * S, U8)
-        place_scale_rows(nc.sync, bc_scales[:], bc_rows[:])
-        wb_raw = placed("wb_raw", PASSES * H, I32, WB_AT)
-        nc.sync.dma_start(
-            wb_raw[:].rearrange("p (a w) -> p a w", a=PASSES),
-            wb_words.rearrange("a p e i -> a p (e i)").bitcast(I32).rearrange("a p w -> p a w"),
-        )
-        bias = placed("bias", PACK, F32, BIAS_AT)
-        nc.sync.dma_start(bias[:], bf.rearrange("(p t) -> p t", t=PACK))
-        wf_raw = placed("wf_raw", PACK * N, F32, WF_AT)
-        wf_rows = wf.rearrange("(q t i) n -> t q i n", t=PACK, i=8)
-        for t in range(PACK):
-            nc.sync.dma_start(wf_raw[:, t * N : (t + 1) * N], wf_rows[t])
 
         wc_bf = [kept(f"wc_bf{a}", PACK * H, BF16) for a in range(PASSES)]
         for a in range(PASSES):
@@ -132,6 +122,12 @@ def tile_list_triplex_median_fault_kernel(
             src = wc_raw[a][:].rearrange("p (j q t u i) -> p u q t j i", t=PACK, u=2, i=4, j=PACK)
             for u in range(2):
                 nc.scalar.copy(dst[:, u], src[:, u])
+        bc_scales = placed("bc_scales", PASSES * 2 * S, U8, WC1_AT)
+        place_scale_rows(nc.scalar, bc_scales[:], bc_rows[:])
+        wf_raw = placed("wf_raw", PACK * N, F32, WF_AT)
+        wf_rows = wf.rearrange("(q t i) n -> t q i n", t=PACK, i=8)
+        for t in range(PACK):
+            nc.sync.dma_start(wf_raw[:, t * N : (t + 1) * N], wf_rows[t])
 
         words = {}
 
@@ -210,6 +206,7 @@ def tile_list_triplex_median_fault_kernel(
         gather(B, 0, 0)
         gather(A, 0, 1)
         gather(C, 0, 1)
+        gather(B, 0, 1)
         for a in range(PASSES):
             nc.vector.quantize_mx(out=wc_codes[a][:].bitcast(FP8X4), scales=wc_scales[a][:], in_=wc_bf[a][:])
         gather(A, 1, 0)
@@ -223,7 +220,6 @@ def tile_list_triplex_median_fault_kernel(
         project(A, 1)
         gather(C, 1, 1, at=LAST_C_AT)
         project(C, 1)
-        gather(B, 0, 1, at=WB_AT)
         gather(B, 1, 1)
         project(B, 1, emptied=False)
         wf_bf = placed("wf_bf", PACK * N, BF16, LAST_C_AT)

@@ -31,7 +31,10 @@ A, B, C = 0, 1, 2
 
 WC1_AT = 0
 WF_AT = WC1_AT + 4 * PACK * H
-LAST_C_AT = WF_AT + 4 * PACK * N
+WB_AT = WF_AT + 4 * PACK * N
+WC1_BF_AT = WB_AT + 4 * PASSES * H
+FIRST_B_AT = WC1_BF_AT + 2 * PACK * H
+A_AT = FIRST_B_AT + 2 * PACK * N
 
 
 def tile_list_triplex_median_fault_kernel(
@@ -91,7 +94,7 @@ def tile_list_triplex_median_fault_kernel(
             nc.sync.dma_start(wc_raw[a][:], wc[512 * a : 512 * (a + 1), :].rearrange("(p j) r -> p (j r)", j=PACK))
         word_win.append(kept("word_win1", T, I32))
         load_words(word_win[1], 1)
-        wb_raw = kept("wb_raw", PASSES * H, I32)
+        wb_raw = placed("wb_raw", PASSES * H, I32, WB_AT)
         nc.sync.dma_start(
             wb_raw[:].rearrange("p (a w) -> p a w", a=PASSES),
             wb_words.rearrange("a p e i -> a p (e i)").bitcast(I32).rearrange("a p w -> p a w"),
@@ -116,7 +119,7 @@ def tile_list_triplex_median_fault_kernel(
         for x in (C, B):
             nc.vector.tensor_copy(bc_rows[:, (x - 1) * S : x * S], scale_win[:].indirect(lists[x][:]))
 
-        wc_bf = [kept(f"wc_bf{a}", PACK * H, BF16) for a in range(PASSES)]
+        wc_bf = [kept("wc_bf0", PACK * H, BF16), placed("wc_bf1", PACK * H, BF16, WC1_BF_AT)]
         for a in range(PASSES):
             dst = wc_bf[a][:].rearrange("p (t q u i j) -> p u q t j i", t=PACK, u=2, i=4, j=PACK)
             src = wc_raw[a][:].rearrange("p (j q t u i) -> p u q t j i", t=PACK, u=2, i=4, j=PACK)
@@ -155,7 +158,7 @@ def tile_list_triplex_median_fault_kernel(
                 return wb_codes[:, lo : lo + P].bitcast(FP8X4), first_scales[:, s0 : s0 + P]
             return wc_codes[a][:, t * P : (t + 1) * P].bitcast(FP8X4), wc_scales[a][:, t * P : (t + 1) * P]
 
-        sums = [[kept(f"sum{x}_{half}", PACK * HALF, BF16) for half in range(2 - (x == B))] for x in range(3)]
+        sums = [[kept(f"sum{x}_{half}", PACK * HALF, BF16) for half in range(2)] for x in range(3)]
         banks = {}
 
         def multiply(x, a, half, blk):
@@ -163,7 +166,7 @@ def tile_list_triplex_median_fault_kernel(
             width = HALF // len(slices)
             if a == 0:
                 banks[x, half, blk] = psum.tile(
-                    [P, len(slices), width], F32, name=f"bank{(half + (x == C)) % 2 * BANKS + blk}"
+                    [P, len(slices), width], F32, name=f"bank{(half, 1, 0)[x] * BANKS + blk}"
                 )
             bank = banks[x, half, blk]
             j0 = blk * BLOCK // width * width
@@ -200,33 +203,39 @@ def tile_list_triplex_median_fault_kernel(
                 if a == PASSES - 1:
                     empty(x, half, blk)
 
-        gather(A, 0, 0)
-        run_pass(A, 0, 0)
-        gather(C, 0, 0)
-        gather(B, 0, 0)
-        gather(A, 0, 1)
-        gather(C, 0, 1)
-        gather(B, 0, 1)
-        for a in range(PASSES):
+        def quantise_wc(a):
             nc.vector.quantize_mx(out=wc_codes[a][:].bitcast(FP8X4), scales=wc_scales[a][:], in_=wc_bf[a][:])
-        gather(A, 1, 0)
-        run_pass(A, 1, 0)
+
+        gather(A, 0, 0, halves=2)
+        for half in range(2):
+            run_pass(A, 0, half)
+        gather(C, 0, 0)
+        quantise_wc(0)
+        for half in range(2):
+            gather(A, 1, half, at=A_AT + 4 * HALF * half)
+            run_pass(A, 1, half)
+        quantise_wc(1)
         gather(C, 1, 0)
         project(C, 0)
-        gather(B, 1, 0)
+        gather(B, 0, 0, at=WC1_BF_AT)
         deal(wb_codes[:], wb_raw[:], 8)
+        gather(B, 1, 0, at=FIRST_B_AT)
         project(B, 0)
-        gather(A, 1, 1)
-        project(A, 1)
-        gather(C, 1, 1, at=LAST_C_AT)
-        project(C, 1)
-        gather(B, 1, 1)
-        project(B, 1, emptied=False)
-        wf_bf = placed("wf_bf", PACK * N, BF16, LAST_C_AT)
+        wf_bf = placed("wf_bf", PACK * N, BF16, FIRST_B_AT)
         nc.scalar.copy(
             wf_bf[:].rearrange("p (t m j) -> p m j t", t=PACK, j=PACK),
             wf_raw[:].rearrange("p (j m t) -> p m j t", t=PACK, j=PACK),
         )
+        gather(C, 0, 1, at=WB_AT)
+        gather(C, 1, 1, at=WB_AT + 4 * HALF)
+        gather(B, 0, 1, at=A_AT + 4 * HALF)
+        gather(B, 1, 1, at=WC1_BF_AT + 4 * HALF)
+        for x in (C, B):
+            project(x, 1, emptied=False)
+        for quarter in range(2):
+            for x in (C, B):
+                for pair in range(2):
+                    empty(x, 1, 2 * quarter + pair)
 
         highs = [kept(f"high{half}", PACK * HALF, BF16) for half in range(2)]
         lows = [kept(f"low{half}", PACK * HALF, BF16) for half in range(2)]
@@ -251,15 +260,6 @@ def tile_list_triplex_median_fault_kernel(
         def bounds(j0, width):
             pick(highs, sums[A], sums[C], MAX, j0, width)
             pick(lows, sums[A], sums[C], MIN, j0, width)
-
-        def clip_bank(blk):
-            j0 = HALF + blk // 2 * QUARTER
-            nc.vector.tensor_tensor(
-                part(clips, j0, QUARTER).rearrange("p (u j e) -> p u j e", u=2, e=2)[:, blk % 2],
-                banks[B, 1, blk][:].rearrange("p e j -> p j e"),
-                part(highs, j0, QUARTER).rearrange("p (u j e) -> p u j e", u=2, e=2)[:, blk % 2],
-                MIN,
-            )
 
         def clip(j0):
             pick(clips, highs, sums[B], MIN, j0, QUARTER)
@@ -317,30 +317,28 @@ def tile_list_triplex_median_fault_kernel(
                 out=y_codes[half][:, off : off + width].bitcast(FP8X4), scales=y_scales[:, j0 : j0 + width],
                 in_=part(y_bf, j0, width),
             )
-            if off + width == HALF:
-                nc.sync.dma_start(y_words[:, half * HALF : (half + 1) * HALF], y_codes[half][:].bitcast(I32))
+            nc.sync.dma_start(y_words[:, j0 : j0 + width], y_codes[half][:, off : off + width].bitcast(I32))
 
         bounds(0, HALF)
+        nc.vector.quantize_mx(out=wf_codes[:].bitcast(FP8X4), scales=wf_scales[:], in_=wf_bf[:])
         clip(0)
         clip(256)
         median(0, 256)
         median(256, 256)
         quantise_h(0, 256)
         quantise_h(256, 256)
-        bounds(512, 256)
-        bounds(768, 256)
-        clip_bank(0)
-        clip_bank(1)
-        nc.vector.quantize_mx(out=wf_codes[:].bitcast(FP8X4), scales=wf_scales[:], in_=wf_bf[:])
         score(0, HALF, 0)
-        clip_bank(2)
-        clip_bank(3)
+        bounds(512, 256)
+        clip(512)
+        pick(highs, sums[A], sums[C], MAX, 768, 256)
         median(512, 256)
-        median(768, 128)
+        pick(lows, sums[A], sums[C], MIN, 768, 256)
         quantise_h(512, 256)
+        score(512, 256, 4)
+        clip(768)
+        median(768, 128)
         median(896, 128)
         quantise_h(768, 128)
-        score(512, 256, 4)
         quantise_h(896, 128)
         score(768, 128, 6)
         score(896, 128, 0)

@@ -209,7 +209,7 @@ def tile_list_triplex_median_fault_kernel(
         gather(A, 0, 0, halves=2)
         for half in range(2):
             run_pass(A, 0, half)
-        gather(C, 0, 0)
+        gather(C, 0, 0, halves=2)
         quantise_wc(0)
         for half in range(2):
             gather(A, 1, half, at=A_AT + 4 * HALF * half)
@@ -226,10 +226,9 @@ def tile_list_triplex_median_fault_kernel(
             wf_bf[:].rearrange("p (t m j) -> p m j t", t=PACK, j=PACK),
             wf_raw[:].rearrange("p (j m t) -> p m j t", t=PACK, j=PACK),
         )
-        gather(C, 0, 1, at=WB_AT)
-        gather(C, 1, 1, at=WB_AT + 4 * HALF)
+        gather(C, 1, 1, at=WB_AT)
         gather(B, 0, 1, at=A_AT + 4 * HALF)
-        gather(B, 1, 1, at=WC1_BF_AT + 4 * HALF)
+        gather(B, 1, 1, at=WB_AT + 4 * HALF)
         for x in (C, B):
             project(x, 1, emptied=False)
         for quarter in range(2):

@@ -32,9 +32,7 @@ A, B, C = 0, 1, 2
 WC1_AT = 0
 WF_AT = WC1_AT + 4 * PACK * H
 WB_AT = WF_AT + 4 * PACK * N
-WC1_BF_AT = WB_AT + 4 * PASSES * H
-FIRST_B_AT = WC1_BF_AT + 2 * PACK * H
-A_AT = FIRST_B_AT + 2 * PACK * N
+FIRST_B_AT = WB_AT + 4 * PASSES * H
 
 
 def tile_list_triplex_median_fault_kernel(
@@ -76,8 +74,8 @@ def tile_list_triplex_median_fault_kernel(
                 src.rearrange("p (a q t w) -> p a t q w", a=2, t=PACK, w=run),
             )
 
-        nc.sync.dma_start(lists[A][:], offs)
         load_scale_rows(nc.sync, scale_win[:], tab_scales)
+        nc.sync.dma_start(lists[A][:], offs)
         load_scale_rows(nc.scalar, ws_raw[:, 0:H], wa_scales)
         load_scale_rows(nc.scalar, ws_raw[:, H : 2 * H], wb_scales)
         nc.sync.dma_start(lists[B][:], offs2)
@@ -119,9 +117,9 @@ def tile_list_triplex_median_fault_kernel(
         for x in (C, B):
             nc.vector.tensor_copy(bc_rows[:, (x - 1) * S : x * S], scale_win[:].indirect(lists[x][:]))
 
-        wc_bf = [kept("wc_bf0", PACK * H, BF16), placed("wc_bf1", PACK * H, BF16, WC1_BF_AT)]
+        wc_bf = kept("wc_bf", PASSES * PACK * H, BF16)
         for a in range(PASSES):
-            dst = wc_bf[a][:].rearrange("p (t q u i j) -> p u q t j i", t=PACK, u=2, i=4, j=PACK)
+            dst = wc_bf[:, a * PACK * H : (a + 1) * PACK * H].rearrange("p (t q u i j) -> p u q t j i", t=PACK, u=2, i=4, j=PACK)
             src = wc_raw[a][:].rearrange("p (j q t u i) -> p u q t j i", t=PACK, u=2, i=4, j=PACK)
             for u in range(2):
                 nc.scalar.copy(dst[:, u], src[:, u])
@@ -144,8 +142,8 @@ def tile_list_triplex_median_fault_kernel(
                 words[x, a, half + e] = g[:, e * HALF : (e + 1) * HALF]
 
         wb_codes = kept("wb_codes", PASSES * H, I32)
-        wc_codes = [kept(f"wc_codes{a}", H, U32) for a in range(PASSES)]
-        wc_scales = [kept(f"wc_scales{a}", H, U8) for a in range(PASSES)]
+        wc_codes = kept("wc_codes", PASSES * H, U32)
+        wc_scales = kept("wc_scales", PASSES * H, U8)
         wf_codes = kept("wf_codes", N, U32)
         wf_scales = kept("wf_scales", N, U8)
 
@@ -156,7 +154,7 @@ def tile_list_triplex_median_fault_kernel(
                 return wa_codes[:, 2 * lo : 2 * (lo + P)].bitcast(FP4X4), first_scales[:, s0 : s0 + P]
             if x == B:
                 return wb_codes[:, lo : lo + P].bitcast(FP8X4), first_scales[:, s0 : s0 + P]
-            return wc_codes[a][:, t * P : (t + 1) * P].bitcast(FP8X4), wc_scales[a][:, t * P : (t + 1) * P]
+            return wc_codes[:, lo : lo + P].bitcast(FP8X4), wc_scales[:, lo : lo + P]
 
         sums = [[kept(f"sum{x}_{half}", PACK * HALF, BF16) for half in range(2)] for x in range(3)]
         banks = {}
@@ -186,7 +184,7 @@ def tile_list_triplex_median_fault_kernel(
             if x == A:
                 j0 = blk % 2 * BLOCK
                 src = banks[x, half, blk][:].rearrange("p (u e) j -> p u j e", u=2)
-                nc.scalar.activation(dst[:, :, j0 : j0 + BLOCK, :], src, IDENTITY)
+                nc.scalar.copy(dst[:, :, j0 : j0 + BLOCK, :], src)
             else:
                 nc.scalar.copy(dst[:, blk % 2], banks[x, half, blk][:].rearrange("p e j -> p j e"))
 
@@ -203,21 +201,17 @@ def tile_list_triplex_median_fault_kernel(
                 if a == PASSES - 1:
                     empty(x, half, blk)
 
-        def quantise_wc(a):
-            nc.vector.quantize_mx(out=wc_codes[a][:].bitcast(FP8X4), scales=wc_scales[a][:], in_=wc_bf[a][:])
-
         gather(A, 0, 0, halves=2)
         for half in range(2):
             run_pass(A, 0, half)
         gather(C, 0, 0, halves=2)
-        quantise_wc(0)
+        gather(B, 0, 0)
+        nc.vector.quantize_mx(out=wc_codes[:].bitcast(FP8X4), scales=wc_scales[:], in_=wc_bf[:])
         for half in range(2):
-            gather(A, 1, half, at=A_AT + 4 * HALF * half)
+            gather(A, 1, half)
             run_pass(A, 1, half)
-        quantise_wc(1)
-        gather(C, 1, 0)
+        gather(C, 1, 0, halves=2)
         project(C, 0)
-        gather(B, 0, 0, at=WC1_BF_AT)
         deal(wb_codes[:], wb_raw[:], 8)
         gather(B, 1, 0, at=FIRST_B_AT)
         project(B, 0)
@@ -226,9 +220,8 @@ def tile_list_triplex_median_fault_kernel(
             wf_bf[:].rearrange("p (t m j) -> p m j t", t=PACK, j=PACK),
             wf_raw[:].rearrange("p (j m t) -> p m j t", t=PACK, j=PACK),
         )
-        gather(C, 1, 1, at=WB_AT)
-        gather(B, 0, 1, at=A_AT + 4 * HALF)
-        gather(B, 1, 1, at=WB_AT + 4 * HALF)
+        for a in range(PASSES):
+            gather(B, a, 1, at=WB_AT + 4 * HALF * a)
         for x in (C, B):
             project(x, 1, emptied=False)
         for quarter in range(2):

@@ -339,7 +339,7 @@ def tile_list_triplex_median_fault_kernel(
         planes(0, HALF)
         weave(nc.vector.tensor_copy, 768, 128)
         planes(512, 256)
-        weave(nc.vector.tensor_copy, 896, 128)
+        weave(nc.scalar.copy, 896, 128)
         planes(768, 256)
         for q in range(QUADS):
             eng = nc.scalar if q % 2 else nc.sync

@@ -23,16 +23,21 @@ PASSES = K // (P * PACK)
 HALF = S // 2
 QUARTER = S // 4
 BLOCK = 128
-BANKS = HALF // BLOCK
+BANKS = 4
 QUADS = 4
 ROWS = 32
 FIRST = 2 * H + S
 A, B, C = 0, 1, 2
+PLANE_ROW = {A: 0, B: 4, C: 8}
 
-WC1_AT = 0
-WF_AT = WC1_AT + 4 * PACK * H
-WB_AT = WF_AT + 4 * PACK * N
-FIRST_B_AT = WB_AT + 4 * PASSES * H
+SUM_C_AT = 0
+WB_AT = 2048
+SECOND_AT = WB_AT + 4 * PASSES * H
+A_ROWS_AT = SECOND_AT - S // 2
+WA_AT = SECOND_AT + 4 * T
+WC1_AT = WA_AT + PASSES * FIRST
+BIAS_AT = WC1_AT + PASSES * S
+WF_AT = BIAS_AT + 64
 
 
 def tile_list_triplex_median_fault_kernel(
@@ -58,18 +63,21 @@ def tile_list_triplex_median_fault_kernel(
         def load_scale_rows(eng, dst, src):
             eng.dma_start(dst[0:ROWS, :].bitcast(I32), src.rearrange("a q t -> q a t").bitcast(I32))
 
-        def place_scale_rows(eng, dst, src):
+        def place_scale_rows(eng, dst, src, row):
             for q in (0, 2, 1, 3):
                 eng.dma_start(
-                    dst[32 * q : 32 * q + 4, :].bitcast(I32).rearrange("r (a w) -> r a w", a=PASSES),
+                    dst[32 * q + row : 32 * q + row + 4, :].bitcast(I32).rearrange("r (a w) -> r a w", a=PASSES),
                     src[8 * q : 8 * q + 8, :].bitcast(I32),
                 )
 
         def load_words(win, a):
             nc.sync.dma_start(win[:], tab_words[a].rearrange("p t i -> p (t i)").bitcast(I32))
 
-        def deal(dst, src, run):
-            nc.vector.tensor_copy(
+        def load_wc(raw, a):
+            nc.sync.dma_start(raw[:], wc[512 * a : 512 * (a + 1), :].rearrange("(p j) r -> p (j r)", j=PACK))
+
+        def deal(copy, dst, src, run):
+            copy(
                 dst.rearrange("p (a t q w) -> p a t q w", a=2, t=PACK, w=run),
                 src.rearrange("p (a q t w) -> p a t q w", a=2, t=PACK, w=run),
             )
@@ -78,57 +86,65 @@ def tile_list_triplex_median_fault_kernel(
         nc.sync.dma_start(lists[A][:], offs)
         load_scale_rows(nc.scalar, ws_raw[:, 0:H], wa_scales)
         load_scale_rows(nc.scalar, ws_raw[:, H : 2 * H], wb_scales)
-        nc.sync.dma_start(lists[B][:], offs2)
         nc.sync.dma_start(lists[C][:], offs3)
-        wa_raw = kept("wa_raw", PASSES * 2 * H, U8)
+        nc.sync.dma_start(lists[B][:], offs2)
+        wc_raw = [kept("wc_raw0", PACK * H, F32), placed("wc_raw1", PACK * H, F32, WC1_AT)]
+        word_win = [kept("word_win0", T, I32)]
+        wa_raw = placed("wa_raw", PASSES * 2 * H, U8, WA_AT)
+        load_wc(wc_raw[0], 0)
         nc.sync.dma_start(
             wa_raw[:].bitcast(I32).rearrange("p (a w) -> p a w", a=PASSES),
             wa_words.bitcast(I32).rearrange("a p w -> p a w"),
         )
-        word_win = [kept("word_win0", T, I32)]
         load_words(word_win[0], 0)
-        wc_raw = [kept("wc_raw0", PACK * H, F32), placed("wc_raw1", PACK * H, F32, WC1_AT)]
-        for a in range(PASSES):
-            nc.sync.dma_start(wc_raw[a][:], wc[512 * a : 512 * (a + 1), :].rearrange("(p j) r -> p (j r)", j=PACK))
-        word_win.append(kept("word_win1", T, I32))
+        load_wc(wc_raw[1], 1)
+
+        nc.vector.memset(scale_win[32:64, :].bitcast(I32), 0)
+        nc.vector.memset(scale_win[64:P, :].bitcast(I32), 0)
+
+        wc_bf = kept("wc_bf", PASSES * PACK * H, BF16)
+        wa_codes = kept("wa_codes", PASSES * 2 * H, U8)
+        first_rows = kept("first_rows", FIRST, U8)
+
+        def round_wc(a):
+            dst = wc_bf[:, a * PACK * H : (a + 1) * PACK * H].rearrange("p (t q u i j) -> p u q t j i", t=PACK, u=2, i=4, j=PACK)
+            src = wc_raw[a][:].rearrange("p (j q t u i) -> p u q t j i", t=PACK, u=2, i=4, j=PACK)
+            for u in range(2):
+                nc.scalar.copy(dst[:, u], src[:, u])
+
+        deal(nc.scalar.copy, first_rows[0:ROWS, 0 : 2 * H].bitcast(U32), ws_raw[0:ROWS, :].bitcast(U32), 2)
+        round_wc(0)
+        deal(nc.scalar.copy, wa_codes[:].bitcast(U32), wa_raw[:].bitcast(U32), 4)
+        round_wc(1)
+
+        c_rows = kept("c_rows", S, U8)
+        a_rows = placed("a_rows", S, U8, A_ROWS_AT)
+        b_rows = kept("b_rows", S, U8)
+        c_scales = kept("c_scales", PASSES * S, U8)
+        nc.vector.tensor_copy(a_rows[:], scale_win[:].indirect(lists[A][:]))
+        nc.vector.tensor_copy(c_rows[:], scale_win[:].indirect(lists[C][:]))
+        place_scale_rows(nc.sync, c_scales[:], c_rows[:], PLANE_ROW[C])
+        nc.vector.tensor_copy(first_rows[0:ROWS, 2 * H : FIRST].bitcast(I32), a_rows[0:ROWS, :].bitcast(I32))
+        nc.vector.tensor_copy(b_rows[:], scale_win[:].indirect(lists[B][:]))
+        word_win.append(placed("word_win1", T, I32, SECOND_AT))
         load_words(word_win[1], 1)
         wb_raw = placed("wb_raw", PASSES * H, I32, WB_AT)
         nc.sync.dma_start(
             wb_raw[:].rearrange("p (a w) -> p a w", a=PASSES),
             wb_words.rearrange("a p e i -> a p (e i)").bitcast(I32).rearrange("a p w -> p a w"),
         )
-        bias = kept("bias", PACK, F32)
-        nc.sync.dma_start(bias[:], bf.rearrange("(p t) -> p t", t=PACK))
-
-        nc.vector.memset(scale_win[32:64, :].bitcast(I32), 0)
-        nc.vector.memset(scale_win[64:P, :].bitcast(I32), 0)
-
-        a_rows = kept("a_rows", S, U8)
-        first_rows = kept("first_rows", FIRST, U8)
-        first_scales = kept("first_scales", PASSES * FIRST, U8)
-        nc.vector.tensor_copy(a_rows[:], scale_win[:].indirect(lists[A][:]))
-        deal(first_rows[0:ROWS, 0 : 2 * H].bitcast(I32), ws_raw[0:ROWS, :].bitcast(I32), 2)
-        nc.vector.tensor_copy(first_rows[0:ROWS, 2 * H : FIRST].bitcast(I32), a_rows[0:ROWS, :].bitcast(I32))
-        place_scale_rows(nc.scalar, first_scales[:], first_rows[:])
-        wa_codes = kept("wa_codes", PASSES * 2 * H, U8)
-        deal(wa_codes[:].bitcast(I32), wa_raw[:].bitcast(I32), 4)
-
-        bc_rows = placed("bc_rows", 2 * S, U8, WF_AT)
-        for x in (C, B):
-            nc.vector.tensor_copy(bc_rows[:, (x - 1) * S : x * S], scale_win[:].indirect(lists[x][:]))
-
-        wc_bf = kept("wc_bf", PASSES * PACK * H, BF16)
-        for a in range(PASSES):
-            dst = wc_bf[:, a * PACK * H : (a + 1) * PACK * H].rearrange("p (t q u i j) -> p u q t j i", t=PACK, u=2, i=4, j=PACK)
-            src = wc_raw[a][:].rearrange("p (j q t u i) -> p u q t j i", t=PACK, u=2, i=4, j=PACK)
-            for u in range(2):
-                nc.scalar.copy(dst[:, u], src[:, u])
-        bc_scales = placed("bc_scales", PASSES * 2 * S, U8, WC1_AT)
-        place_scale_rows(nc.scalar, bc_scales[:], bc_rows[:])
+        first_scales = placed("first_scales", PASSES * FIRST, U8, WA_AT)
+        place_scale_rows(nc.sync, first_scales[:], first_rows[:], PLANE_ROW[A])
+        b_scales = placed("b_scales", PASSES * S, U8, WC1_AT)
+        place_scale_rows(nc.sync, b_scales[:], b_rows[:], PLANE_ROW[B])
         wf_raw = placed("wf_raw", PACK * N, F32, WF_AT)
         wf_rows = wf.rearrange("(q t i) n -> t q i n", t=PACK, i=8)
         for t in range(PACK):
             nc.sync.dma_start(wf_raw[:, t * N : (t + 1) * N], wf_rows[t])
+        bias = placed("bias", PACK, F32, BIAS_AT)
+        nc.sync.dma_start(bias[:], bf.rearrange("(p t) -> p t", t=PACK))
+        wb_codes = kept("wb_codes", PASSES * H, U32)
+        deal(nc.scalar.copy, wb_codes[:], wb_raw[:].bitcast(U32), 8)
 
         words = {}
 
@@ -141,7 +157,6 @@ def tile_list_triplex_median_fault_kernel(
             for e in range(halves):
                 words[x, a, half + e] = g[:, e * HALF : (e + 1) * HALF]
 
-        wb_codes = kept("wb_codes", PASSES * H, I32)
         wc_codes = kept("wc_codes", PASSES * H, U32)
         wc_scales = kept("wc_scales", PASSES * H, U8)
         wf_codes = kept("wf_codes", N, U32)
@@ -156,37 +171,33 @@ def tile_list_triplex_median_fault_kernel(
                 return wb_codes[:, lo : lo + P].bitcast(FP8X4), first_scales[:, s0 : s0 + P]
             return wc_codes[:, lo : lo + P].bitcast(FP8X4), wc_scales[:, lo : lo + P]
 
-        sums = [[kept(f"sum{x}_{half}", PACK * HALF, BF16) for half in range(2)] for x in range(3)]
+        def moving_scales(x, a, j0):
+            if x == A:
+                s0 = a * FIRST + 2 * H + j0
+                return first_scales[:, s0 : s0 + QUARTER]
+            plane = b_scales if x == B else c_scales
+            return plane[PLANE_ROW[x] : P, a * S + j0 : a * S + j0 + QUARTER]
+
+        sums = [[kept(f"sum{x}_{half}", PACK * HALF, BF16) for half in range(2)] for x in (A, B)]
+        sums.append([placed("sum2_0", PACK * HALF, BF16, SUM_C_AT), kept("sum2_1", PACK * HALF, BF16)])
         banks = {}
 
         def multiply(x, a, half, blk):
-            slices = range(PACK) if x == A else range(2 * (blk % 2), 2 * (blk % 2) + 2)
-            width = HALF // len(slices)
             if a == 0:
-                banks[x, half, blk] = psum.tile(
-                    [P, len(slices), width], F32, name=f"bank{(half, 1, 0)[x] * BANKS + blk}"
-                )
-            bank = banks[x, half, blk]
-            j0 = blk * BLOCK // width * width
-            s0 = half * HALF + j0 + (a * FIRST + 2 * H if x == A else (2 * a + x - 1) * S)
-            plane = first_scales if x == A else bc_scales
-            for e, t in enumerate(slices):
-                codes, scales = stationary(x, a, t)
+                banks[x, half, blk] = psum.tile([P, 2, QUARTER], F32, name=f"bank{(1 - half, half, half)[x] * BANKS + blk}")
+            j0 = blk // 2 * QUARTER
+            for e in range(2):
+                codes, scales = stationary(x, a, 2 * (blk % 2) + e)
                 nc.tensor.matmul_mx(
-                    out=bank[:, e, :], lhsT=codes, lhsT_scale=scales,
-                    rhs=words[x, a, half][:, j0 : j0 + width].bitcast(FP8X4),
-                    rhs_scale=plane[:, s0 : s0 + width],
-                    start=(a == 0 and e == 0), stop=(a == PASSES - 1 and e == len(slices) - 1),
+                    out=banks[x, half, blk][:, e, :], lhsT=codes, lhsT_scale=scales,
+                    rhs=words[x, a, half][:, j0 : j0 + QUARTER].bitcast(FP8X4),
+                    rhs_scale=moving_scales(x, a, half * HALF + j0),
+                    start=(a == 0 and e == 0), stop=(a == PASSES - 1 and e == 1),
                 )
 
         def empty(x, half, blk):
-            dst = sums[x][half][:].rearrange("p (c u j e) -> p c u j e", c=2, u=2, e=2)[:, blk // 2]
-            if x == A:
-                j0 = blk % 2 * BLOCK
-                src = banks[x, half, blk][:].rearrange("p (u e) j -> p u j e", u=2)
-                nc.scalar.copy(dst[:, :, j0 : j0 + BLOCK, :], src)
-            else:
-                nc.scalar.copy(dst[:, blk % 2], banks[x, half, blk][:].rearrange("p e j -> p j e"))
+            dst = sums[x][half][:].rearrange("p (b j e) -> p b j e", b=BANKS, e=2)[:, blk]
+            nc.scalar.copy(dst, banks[x, half, blk][:].rearrange("p e j -> p j e"))
 
         def project(x, half, emptied=True):
             for blk in range(BANKS):
@@ -201,31 +212,32 @@ def tile_list_triplex_median_fault_kernel(
                 if a == PASSES - 1:
                     empty(x, half, blk)
 
-        gather(A, 0, 0, halves=2)
-        for half in range(2):
-            run_pass(A, 0, half)
+        def quantise_wc(a):
+            nc.vector.quantize_mx(
+                out=wc_codes[:, a * H : (a + 1) * H].bitcast(FP8X4), scales=wc_scales[:, a * H : (a + 1) * H],
+                in_=wc_bf[:, a * PACK * H : (a + 1) * PACK * H],
+            )
+
+        quantise_wc(0)
         gather(C, 0, 0, halves=2)
+        run_pass(C, 0, 0)
+        gather(A, 0, 0, halves=2)
         gather(B, 0, 0)
-        nc.vector.quantize_mx(out=wc_codes[:].bitcast(FP8X4), scales=wc_scales[:], in_=wc_bf[:])
-        for half in range(2):
-            gather(A, 1, half)
-            run_pass(A, 1, half)
-        gather(C, 1, 0, halves=2)
-        project(C, 0)
-        deal(wb_codes[:], wb_raw[:], 8)
-        gather(B, 1, 0, at=FIRST_B_AT)
-        project(B, 0)
-        wf_bf = placed("wf_bf", PACK * N, BF16, FIRST_B_AT)
-        nc.scalar.copy(
-            wf_bf[:].rearrange("p (t m j) -> p m j t", t=PACK, j=PACK),
-            wf_raw[:].rearrange("p (j m t) -> p m j t", t=PACK, j=PACK),
-        )
-        for a in range(PASSES):
-            gather(B, a, 1, at=WB_AT + 4 * HALF * a)
-        for x in (C, B):
+        quantise_wc(1)
+        gather(C, 1, 0)
+        run_pass(C, 1, 0)
+        for x in (A, B):
+            gather(x, 1, 0)
+            project(x, 0)
+        gather(C, 1, 1)
+        project(C, 1)
+        gather(A, 1, 1)
+        gather(B, 0, 1, at=WB_AT + 4 * HALF)
+        gather(B, 1, 1)
+        for x in (A, B):
             project(x, 1, emptied=False)
         for quarter in range(2):
-            for x in (C, B):
+            for x in (A, B):
                 for pair in range(2):
                     empty(x, 1, 2 * quarter + pair)
 
@@ -272,11 +284,11 @@ def tile_list_triplex_median_fault_kernel(
                 in_=part(medians, j0, width),
             )
 
-        def score(j0, width, first_bank):
+        def score(j0, width, bank_numbers):
             y = kept(f"y{j0}", PACK * width, F32)
-            per_bank = 1 if width == HALF else 2
-            for n in range(PACK // per_bank):
-                bank = psum.tile([P, per_bank, width], F32, name=f"bank{first_bank + n}")
+            per_bank = PACK // len(bank_numbers)
+            for n, number in enumerate(bank_numbers):
+                bank = psum.tile([P, per_bank, width], F32, name=f"bank{number}")
                 for u in range(per_bank):
                     t = per_bank * n + u
                     nc.tensor.matmul_mx(
@@ -311,29 +323,34 @@ def tile_list_triplex_median_fault_kernel(
             )
             nc.sync.dma_start(y_words[:, j0 : j0 + width], y_codes[half][:, off : off + width].bitcast(I32))
 
+        wf_bf = kept("wf_bf", PACK * N, BF16)
         bounds(0, HALF)
-        nc.vector.quantize_mx(out=wf_codes[:].bitcast(FP8X4), scales=wf_scales[:], in_=wf_bf[:])
+        nc.vector.tensor_copy(
+            wf_bf[:].rearrange("p (t m j) -> p m j t", t=PACK, j=PACK),
+            wf_raw[:].rearrange("p (j m t) -> p m j t", t=PACK, j=PACK),
+        )
         clip(0)
         clip(256)
         median(0, 256)
+        nc.vector.quantize_mx(out=wf_codes[:].bitcast(FP8X4), scales=wf_scales[:], in_=wf_bf[:])
         median(256, 256)
         quantise_h(0, 256)
         quantise_h(256, 256)
-        score(0, HALF, 0)
+        score(0, HALF, (0, 1, 4, 5))
         bounds(512, 256)
         clip(512)
         pick(highs, sums[A], sums[C], MAX, 768, 256)
         median(512, 256)
         pick(lows, sums[A], sums[C], MIN, 768, 256)
         quantise_h(512, 256)
-        score(512, 256, 4)
+        score(512, 256, (2, 3))
         clip(768)
         median(768, 128)
         median(896, 128)
         quantise_h(768, 128)
         quantise_h(896, 128)
-        score(768, 128, 6)
-        score(896, 128, 0)
+        score(768, 128, (6, 7))
+        score(896, 128, (0, 1))
         weave(nc.vector.tensor_copy, 0, HALF)
         weave(nc.vector.tensor_copy, 512, 256)
         planes(0, HALF)

@@ -222,7 +222,7 @@ def tile_list_triplex_median_fault_kernel(
         gather(C, 0, 0, halves=2)
         run_pass(C, 0, 0)
         gather(A, 0, 0, halves=2)
-        gather(B, 0, 0)
+        gather(B, 0, 0, halves=2)
         quantise_wc(1)
         gather(C, 1, 0)
         run_pass(C, 1, 0)
@@ -232,7 +232,6 @@ def tile_list_triplex_median_fault_kernel(
         gather(C, 1, 1)
         project(C, 1)
         gather(A, 1, 1)
-        gather(B, 0, 1, at=WB_AT + 4 * HALF)
         gather(B, 1, 1)
         for x in (A, B):
             project(x, 1, emptied=False)

@@ -283,28 +283,28 @@ def tile_list_triplex_median_fault_kernel(
                 in_=part(medians, j0, width),
             )
 
-        def score(j0, width, bank_numbers):
+        def score(j0, width, bank_numbers, step):
             y = kept(f"y{j0}", PACK * width, F32)
             per_bank = PACK // len(bank_numbers)
-            for n, number in enumerate(bank_numbers):
-                bank = psum.tile([P, per_bank, width], F32, name=f"bank{number}")
-                for u in range(per_bank):
-                    t = per_bank * n + u
+            out_banks = [psum.tile([P, per_bank, width], F32, name=f"bank{number}") for number in bank_numbers]
+            for off in range(0, width, step):
+                cols = slice(j0 + off, j0 + off + step)
+                for t in range(PACK):
                     nc.tensor.matmul_mx(
-                        out=bank[:, u, :], lhsT=wf_codes[:, t * P : (t + 1) * P].bitcast(FP8X4),
+                        out=out_banks[t // per_bank][:, t % per_bank, off : off + step],
+                        lhsT=wf_codes[:, t * P : (t + 1) * P].bitcast(FP8X4),
                         lhsT_scale=wf_scales[:, t * P : (t + 1) * P],
-                        rhs=h_codes[:, j0 : j0 + width].bitcast(FP8X4), rhs_scale=h_scales[:, j0 : j0 + width],
+                        rhs=h_codes[:, cols].bitcast(FP8X4), rhs_scale=h_scales[:, cols],
                         start=True, stop=True,
                     )
+            for n, bank in enumerate(out_banks):
                 for u in range(per_bank):
                     t = per_bank * n + u
                     nc.scalar.activation(
                         y[:, t * width : (t + 1) * width], bank[:, u, :], IDENTITY, bias=bias[:, t : t + 1]
                     )
-                if width == HALF:
-                    nc.sync.dma_start(y_rows[:, n, j0 : j0 + width], y[:, n * width : (n + 1) * width])
-            if width < HALF:
-                nc.sync.dma_start(y_rows[:, :, j0 : j0 + width], y[:].rearrange("p (t j) -> p t j", t=PACK))
+                rows = slice(per_bank * n, per_bank * (n + 1))
+                nc.sync.dma_start(y_rows[:, rows, j0 : j0 + width], y[:].rearrange("p (t j) -> p t j", t=PACK)[:, rows])
             for j in range(j0, j0 + width, BLOCK):
                 scores[j] = y[:].rearrange("p (t j) -> p t j", t=PACK)[:, :, j - j0 :]
 
@@ -335,26 +335,25 @@ def tile_list_triplex_median_fault_kernel(
         median(256, 256)
         quantise_h(0, 256)
         quantise_h(256, 256)
-        score(0, HALF, (0, 1, 4, 5))
+        score(0, HALF, (0, 1, 4, 5), HALF)
         bounds(512, 256)
         clip(512)
         pick(highs, sums[A], sums[C], MAX, 768, 256)
         median(512, 256)
         pick(lows, sums[A], sums[C], MIN, 768, 256)
         quantise_h(512, 256)
-        score(512, 256, (2, 3))
+        score(512, 256, (2, 3), 256)
         clip(768)
         median(768, 128)
         median(896, 128)
         quantise_h(768, 128)
         quantise_h(896, 128)
-        score(768, 128, (6, 7))
-        score(896, 128, (0, 1))
+        score(768, 256, (6, 7), 128)
         weave(nc.vector.tensor_copy, 0, HALF)
         weave(nc.vector.tensor_copy, 512, 256)
         planes(0, HALF)
-        weave(nc.vector.tensor_copy, 768, 128)
         planes(512, 256)
+        weave(nc.vector.tensor_copy, 768, 128)
         weave(nc.scalar.copy, 896, 128)
         planes(768, 256)
         for q in range(QUADS):

@@ -38,6 +38,8 @@ WA_AT = SECOND_AT + 4 * T
 WC1_AT = WA_AT + PASSES * FIRST
 BIAS_AT = WC1_AT + PASSES * S
 WF_AT = BIAS_AT + 64
+WF_BF_AT = WF_AT + 4 * PACK * N
+WF_ON_SCALAR = 32
 
 
 def tile_list_triplex_median_fault_kernel(
@@ -148,12 +150,14 @@ def tile_list_triplex_median_fault_kernel(
 
         words = {}
 
-        def gather(x, a, half, halves=1, at=None):
-            name = "g%d%d%d" % (x, a, half)
+        def gather(x, a, half, halves=1, step=None, at=None):
             width = halves * HALF
+            step = step or width
+            name = "g%d%d%d" % (x, a, half)
             g = kept(name, width, U32) if at is None else placed(name, width, U32, at)
-            cols = slice(half * HALF // 16, (half * HALF + width) // 16)
-            nc.vector.tensor_copy(g[:], word_win[a][:].bitcast(U32).indirect(lists[x][:, cols]))
+            for off in range(0, width, step):
+                cols = slice((half * HALF + off) // 16, (half * HALF + off + step) // 16)
+                nc.vector.tensor_copy(g[:, off : off + step], word_win[a][:].bitcast(U32).indirect(lists[x][:, cols]))
             for e in range(halves):
                 words[x, a, half + e] = g[:, e * HALF : (e + 1) * HALF]
 
@@ -224,11 +228,20 @@ def tile_list_triplex_median_fault_kernel(
         gather(A, 0, 0, halves=2)
         gather(B, 0, 0, halves=2)
         quantise_wc(1)
-        gather(C, 1, 0)
+        gather(C, 1, 0, step=QUARTER)
         run_pass(C, 1, 0)
         for x in (A, B):
-            gather(x, 1, 0)
+            gather(x, 1, 0, at=WF_BF_AT if x == B else None)
             project(x, 0)
+        wf_bf = placed("wf_bf", PACK * N, BF16, WF_BF_AT)
+
+        def round_wf(copy, cols):
+            copy(
+                wf_bf[:].rearrange("p (t m j) -> p m j t", t=PACK, j=PACK)[:, cols],
+                wf_raw[:].rearrange("p (j m t) -> p m j t", t=PACK, j=PACK)[:, cols],
+            )
+
+        round_wf(nc.scalar.copy, slice(0, WF_ON_SCALAR))
         gather(C, 1, 1)
         project(C, 1)
         gather(A, 1, 1)
@@ -322,12 +335,8 @@ def tile_list_triplex_median_fault_kernel(
             )
             nc.sync.dma_start(y_words[:, j0 : j0 + width], y_codes[half][:, off : off + width].bitcast(I32))
 
-        wf_bf = kept("wf_bf", PACK * N, BF16)
         bounds(0, HALF)
-        nc.vector.tensor_copy(
-            wf_bf[:].rearrange("p (t m j) -> p m j t", t=PACK, j=PACK),
-            wf_raw[:].rearrange("p (j m t) -> p m j t", t=PACK, j=PACK),
-        )
+        round_wf(nc.vector.tensor_copy, slice(WF_ON_SCALAR, P))
         clip(0)
         clip(256)
         median(0, 256)

@@ -39,7 +39,6 @@ WC1_AT = WA_AT + PASSES * FIRST
 BIAS_AT = WC1_AT + PASSES * S
 WF_AT = BIAS_AT + 64
 WF_BF_AT = WF_AT + 4 * PACK * N
-WF_ON_SCALAR = 32
 
 
 def tile_list_triplex_median_fault_kernel(
@@ -223,10 +222,10 @@ def tile_list_triplex_median_fault_kernel(
             )
 
         quantise_wc(0)
+        gather(A, 0, 0, halves=2)
         gather(C, 0, 0, halves=2)
         run_pass(C, 0, 0)
-        gather(A, 0, 0, halves=2)
-        gather(B, 0, 0, halves=2)
+        gather(B, 0, 0)
         quantise_wc(1)
         gather(C, 1, 0, step=QUARTER)
         run_pass(C, 1, 0)
@@ -234,17 +233,14 @@ def tile_list_triplex_median_fault_kernel(
             gather(x, 1, 0, at=WF_BF_AT if x == B else None)
             project(x, 0)
         wf_bf = placed("wf_bf", PACK * N, BF16, WF_BF_AT)
-
-        def round_wf(copy, cols):
-            copy(
-                wf_bf[:].rearrange("p (t m j) -> p m j t", t=PACK, j=PACK)[:, cols],
-                wf_raw[:].rearrange("p (j m t) -> p m j t", t=PACK, j=PACK)[:, cols],
-            )
-
-        round_wf(nc.scalar.copy, slice(0, WF_ON_SCALAR))
+        nc.scalar.copy(
+            wf_bf[:].rearrange("p (t m j) -> p m j t", t=PACK, j=PACK),
+            wf_raw[:].rearrange("p (j m t) -> p m j t", t=PACK, j=PACK),
+        )
         gather(C, 1, 1)
         project(C, 1)
         gather(A, 1, 1)
+        gather(B, 0, 1, at=WB_AT + 4 * HALF)
         gather(B, 1, 1)
         for x in (A, B):
             project(x, 1, emptied=False)
@@ -336,7 +332,6 @@ def tile_list_triplex_median_fault_kernel(
             nc.sync.dma_start(y_words[:, j0 : j0 + width], y_codes[half][:, off : off + width].bitcast(I32))
 
         bounds(0, HALF)
-        round_wf(nc.vector.tensor_copy, slice(WF_ON_SCALAR, P))
         clip(0)
         clip(256)
         median(0, 256)

from contextlib import ExitStack

import concourse.mybir as mybir

K, T, S, H, N = 1024, 4096, 1024, 512, 512
FLOPS = 2 * (3 * K * H * S + H * N * S)

F32 = mybir.dt.float32
BF16 = mybir.dt.bfloat16
I32 = mybir.dt.int32
U32 = mybir.dt.uint32
U16 = mybir.dt.uint16
U8 = mybir.dt.uint8
FP8X4 = mybir.dt.float8_e4m3fn_x4
FP4X4 = mybir.dt.float4_e2m1fn_x4
MIN = mybir.AluOpType.min
MAX = mybir.AluOpType.max
IDENTITY = mybir.ActivationFunctionType.Identity

P = 128
PACK = 4
PASSES = K // (P * PACK)
HALF = S // 2
QUARTER = S // 4
BLOCK = 128
BANKS = 4
QUADS = 4
ROWS = 32
FIRST = 2 * H + S
A, B, C = 0, 1, 2
PLANE_ROW = {A: 0, B: 4, C: 8}

SUM_C_AT = 0
WB_AT = 2048
SECOND_AT = WB_AT + 4 * PASSES * H
A_ROWS_AT = SECOND_AT - S // 2
WA_AT = SECOND_AT + 4 * T
WC1_AT = WA_AT + PASSES * FIRST
BIAS_AT = WC1_AT + PASSES * S
WF_AT = BIAS_AT + 64
WF_BF_AT = WF_AT + 4 * PACK * N


def tile_list_triplex_median_fault_kernel(
    tc, tab_words, tab_scales, offs, offs2, offs3, wa_words, wa_scales, wb_words, wb_scales, wc, wf, bf,
    out_0, out_1, out_2,
):
    nc = tc.nc
    with ExitStack() as ctx:
        keep = ctx.enter_context(tc.tile_pool(name="keep", bufs=1))
        shared = ctx.enter_context(tc.tile_pool(name="shared", bufs=1))
        psum = ctx.enter_context(tc.psum_pool(name="psum", bufs=1))

        def kept(name, width, dtype):
            return keep.tile([P, width], dtype, name=name, align_bytes=64)

        def placed(name, width, dtype, offset):
            return shared.tile([P, width], dtype, name=name, offset=offset, align_bytes=64)

        lists = [keep.tile([P, S // 16], U16, name=f"list{x}") for x in range(3)]
        scale_win = kept("scale_win", T, U8)
        ws_raw = kept("ws_raw", 2 * H, U8)

        def load_scale_rows(eng, dst, src):
            eng.dma_start(dst[0:ROWS, :].bitcast(I32), src.rearrange("a q t -> q a t").bitcast(I32))

        def place_scale_rows(eng, dst, src, row):
            for q in (0, 2, 1, 3):
                eng.dma_start(
                    dst[32 * q + row : 32 * q + row + 4, :].bitcast(I32).rearrange("r (a w) -> r a w", a=PASSES),
                    src[8 * q : 8 * q + 8, :].bitcast(I32),
                )

        def load_words(win, a):
            nc.sync.dma_start(win[:], tab_words[a].rearrange("p t i -> p (t i)").bitcast(I32))

        def load_wc(raw, a):
            nc.sync.dma_start(raw[:], wc[512 * a : 512 * (a + 1), :].rearrange("(p j) r -> p (j r)", j=PACK))

        def deal(copy, dst, src, run):
            copy(
                dst.rearrange("p (a t q w) -> p a t q w", a=2, t=PACK, w=run),
                src.rearrange("p (a q t w) -> p a t q w", a=2, t=PACK, w=run),
            )

        load_scale_rows(nc.sync, scale_win[:], tab_scales)
        nc.sync.dma_start(lists[A][:], offs)
        load_scale_rows(nc.scalar, ws_raw[:, 0:H], wa_scales)
        load_scale_rows(nc.scalar, ws_raw[:, H : 2 * H], wb_scales)
        nc.sync.dma_start(lists[C][:], offs3)
        nc.sync.dma_start(lists[B][:], offs2)
        wc_raw = [kept("wc_raw0", PACK * H, F32), placed("wc_raw1", PACK * H, F32, WC1_AT)]
        word_win = [kept("word_win0", T, I32)]
        wa_raw = placed("wa_raw", PASSES * 2 * H, U8, WA_AT)
        load_wc(wc_raw[0], 0)
        nc.sync.dma_start(
            wa_raw[:].bitcast(I32).rearrange("p (a w) -> p a w", a=PASSES),
            wa_words.bitcast(I32).rearrange("a p w -> p a w"),
        )
        load_words(word_win[0], 0)
        load_wc(wc_raw[1], 1)

        nc.vector.memset(scale_win[32:64, :].bitcast(I32), 0)
        nc.vector.memset(scale_win[64:P, :].bitcast(I32), 0)

        wc_bf = kept("wc_bf", PASSES * PACK * H, BF16)
        wa_codes = kept("wa_codes", PASSES * 2 * H, U8)
        first_rows = kept("first_rows", FIRST, U8)

        def round_wc(a):
            dst = wc_bf[:, a * PACK * H : (a + 1) * PACK * H].rearrange("p (t q u i j) -> p u q t j i", t=PACK, u=2, i=4, j=PACK)
            src = wc_raw[a][:].rearrange("p (j q t u i) -> p u q t j i", t=PACK, u=2, i=4, j=PACK)
            for u in range(2):
                nc.scalar.copy(dst[:, u], src[:, u])

        deal(nc.scalar.copy, first_rows[0:ROWS, 0 : 2 * H].bitcast(U32), ws_raw[0:ROWS, :].bitcast(U32), 2)
        round_wc(0)
        deal(nc.scalar.copy, wa_codes[:].bitcast(U32), wa_raw[:].bitcast(U32), 4)
        round_wc(1)

        c_rows = kept("c_rows", S, U8)
        a_rows = placed("a_rows", S, U8, A_ROWS_AT)
        b_rows = kept("b_rows", S, U8)
        c_scales = kept("c_scales", PASSES * S, U8)
        nc.vector.tensor_copy(a_rows[:], scale_win[:].indirect(lists[A][:]))
        nc.vector.tensor_copy(c_rows[:], scale_win[:].indirect(lists[C][:]))
        place_scale_rows(nc.sync, c_scales[:], c_rows[:], PLANE_ROW[C])
        nc.vector.tensor_copy(first_rows[0:ROWS, 2 * H : FIRST].bitcast(I32), a_rows[0:ROWS, :].bitcast(I32))
        nc.vector.tensor_copy(b_rows[:], scale_win[:].indirect(lists[B][:]))
        word_win.append(placed("word_win1", T, I32, SECOND_AT))
        load_words(word_win[1], 1)
        wb_raw = placed("wb_raw", PASSES * H, I32, WB_AT)
        nc.sync.dma_start(
            wb_raw[:].rearrange("p (a w) -> p a w", a=PASSES),
            wb_words.rearrange("a p e i -> a p (e i)").bitcast(I32).rearrange("a p w -> p a w"),
        )
        first_scales = placed("first_scales", PASSES * FIRST, U8, WA_AT)
        place_scale_rows(nc.sync, first_scales[:], first_rows[:], PLANE_ROW[A])
        b_scales = placed("b_scales", PASSES * S, U8, WC1_AT)
        place_scale_rows(nc.sync, b_scales[:], b_rows[:], PLANE_ROW[B])
        wf_raw = placed("wf_raw", PACK * N, F32, WF_AT)
        wf_rows = wf.rearrange("(q t i) n -> t q i n", t=PACK, i=8)
        for t in range(PACK):
            nc.sync.dma_start(wf_raw[:, t * N : (t + 1) * N], wf_rows[t])
        bias = placed("bias", PACK, F32, BIAS_AT)
        nc.sync.dma_start(bias[:], bf.rearrange("(p t) -> p t", t=PACK))
        wb_codes = kept("wb_codes", PASSES * H, U32)
        deal(nc.scalar.copy, wb_codes[:], wb_raw[:].bitcast(U32), 8)

        words = {}

        def gather(x, a, half, halves=1, step=None, at=None):
            width = halves * HALF
            step = step or width
            name = "g%d%d%d" % (x, a, half)
            g = kept(name, width, U32) if at is None else placed(name, width, U32, at)
            for off in range(0, width, step):
                cols = slice((half * HALF + off) // 16, (half * HALF + off + step) // 16)
                nc.vector.tensor_copy(g[:, off : off + step], word_win[a][:].bitcast(U32).indirect(lists[x][:, cols]))
            for e in range(halves):
                words[x, a, half + e] = g[:, e * HALF : (e + 1) * HALF]

        wc_codes = kept("wc_codes", PASSES * H, U32)
        wc_scales = kept("wc_scales", PASSES * H, U8)
        wf_codes = kept("wf_codes", N, U32)
        wf_scales = kept("wf_scales", N, U8)

        def stationary(x, a, t):
            lo = a * H + t * P
            s0 = a * FIRST + x * H + t * P
            if x == A:
                return wa_codes[:, 2 * lo : 2 * (lo + P)].bitcast(FP4X4), first_scales[:, s0 : s0 + P]
            if x == B:
                return wb_codes[:, lo : lo + P].bitcast(FP8X4), first_scales[:, s0 : s0 + P]
            return wc_codes[:, lo : lo + P].bitcast(FP8X4), wc_scales[:, lo : lo + P]

        def moving_scales(x, a, j0):
            if x == A:
                s0 = a * FIRST + 2 * H + j0
                return first_scales[:, s0 : s0 + QUARTER]
            plane = b_scales if x == B else c_scales
            return plane[PLANE_ROW[x] : P, a * S + j0 : a * S + j0 + QUARTER]

        sums = [[kept(f"sum{x}_{half}", PACK * HALF, BF16) for half in range(2)] for x in (A, B)]
        sums.append([placed("sum2_0", PACK * HALF, BF16, SUM_C_AT), kept("sum2_1", PACK * HALF, BF16)])
        banks = {}

        def multiply(x, a, half, blk):
            if a == 0:
                banks[x, half, blk] = psum.tile([P, 2, QUARTER], F32, name=f"bank{(1 - half, half, half)[x] * BANKS + blk}")
            j0 = blk // 2 * QUARTER
            for e in range(2):
                codes, scales = stationary(x, a, 2 * (blk % 2) + e)
                nc.tensor.matmul_mx(
                    out=banks[x, half, blk][:, e, :], lhsT=codes, lhsT_scale=scales,
                    rhs=words[x, a, half][:, j0 : j0 + QUARTER].bitcast(FP8X4),
                    rhs_scale=moving_scales(x, a, half * HALF + j0),
                    start=(a == 0 and e == 0), stop=(a == PASSES - 1 and e == 1),
                )

        def empty(x, half, blk):
            dst = sums[x][half][:].rearrange("p (b j e) -> p b j e", b=BANKS, e=2)[:, blk]
            nc.scalar.copy(dst, banks[x, half, blk][:].rearrange("p e j -> p j e"))

        def project(x, half, emptied=True):
            for blk in range(BANKS):
                for a in range(PASSES):
                    multiply(x, a, half, blk)
                if emptied:
                    empty(x, half, blk)

        def run_pass(x, a, half):
            for blk in range(BANKS):
                multiply(x, a, half, blk)
                if a == PASSES - 1:
                    empty(x, half, blk)

        def quantise_wc(a):
            nc.vector.quantize_mx(
                out=wc_codes[:, a * H : (a + 1) * H].bitcast(FP8X4), scales=wc_scales[:, a * H : (a + 1) * H],
                in_=wc_bf[:, a * PACK * H : (a + 1) * PACK * H],
            )

        quantise_wc(0)
        gather(A, 0, 0, halves=2)
        gather(C, 0, 0, halves=2)
        run_pass(C, 0, 0)
        gather(B, 0, 0)
        quantise_wc(1)
        gather(C, 1, 0, step=QUARTER)
        run_pass(C, 1, 0)
        for x in (A, B):
            gather(x, 1, 0, at=WF_BF_AT if x == B else None)
            project(x, 0)
        wf_bf = placed("wf_bf", PACK * N, BF16, WF_BF_AT)
        nc.scalar.copy(
            wf_bf[:].rearrange("p (t m j) -> p m j t", t=PACK, j=PACK),
            wf_raw[:].rearrange("p (j m t) -> p m j t", t=PACK, j=PACK),
        )
        gather(C, 1, 1)
        project(C, 1)
        gather(A, 1, 1)
        gather(B, 0, 1, at=WB_AT + 4 * HALF)
        gather(B, 1, 1)
        for x in (A, B):
            project(x, 1, emptied=False)
        for quarter in range(2):
            for x in (A, B):
                for pair in range(2):
                    empty(x, 1, 2 * quarter + pair)

        highs = [kept(f"high{half}", PACK * HALF, BF16) for half in range(2)]
        lows = [kept(f"low{half}", PACK * HALF, BF16) for half in range(2)]
        clips = [kept(f"clip{half}", PACK * HALF, BF16) for half in range(2)]
        medians = [kept(f"median{half}", PACK * HALF, BF16) for half in range(2)]
        y_bf = [kept(f"y_bf{half}", PACK * HALF, BF16) for half in range(2)]
        y_codes = [kept(f"y_codes{half}", HALF, U32) for half in range(2)]
        y_scales = kept("y_scales", S, U8)
        h_codes = kept("h_codes", S, U32)
        h_scales = kept("h_scales", S, U8)
        y_rows = out_0.rearrange("(p t) j -> p t j", t=PACK)
        y_words = out_1[0].rearrange("p m i -> p (m i)").bitcast(I32)
        scores = {}

        def part(tiles, j0, width):
            half, off = divmod(j0, HALF)
            return tiles[half][:, PACK * off : PACK * (off + width)]

        def pick(out, in0, in1, op, j0, width):
            nc.vector.tensor_tensor(part(out, j0, width), part(in0, j0, width), part(in1, j0, width), op)

        def bounds(j0, width):
            pick(highs, sums[A], sums[C], MAX, j0, width)
            pick(lows, sums[A], sums[C], MIN, j0, width)

        def clip(j0):
            pick(clips, highs, sums[B], MIN, j0, QUARTER)

        def median(j0, width):
            q0 = j0 // QUARTER * QUARTER
            cols = slice(j0 - q0, j0 - q0 + width)
            nc.vector.tensor_tensor(
                part(medians, j0, width).rearrange("p (j u e) -> p j u e", u=2, e=2),
                part(lows, q0, QUARTER).rearrange("p (u j e) -> p j u e", u=2, e=2)[:, cols],
                part(clips, q0, QUARTER).rearrange("p (u j e) -> p j u e", u=2, e=2)[:, cols],
                MAX,
            )

        def quantise_h(j0, width):
            nc.vector.quantize_mx(
                out=h_codes[:, j0 : j0 + width].bitcast(FP8X4), scales=h_scales[:, j0 : j0 + width],
                in_=part(medians, j0, width),
            )

        def score(j0, width, bank_numbers, step):
            y = kept(f"y{j0}", PACK * width, F32)
            per_bank = PACK // len(bank_numbers)
            out_banks = [psum.tile([P, per_bank, width], F32, name=f"bank{number}") for number in bank_numbers]
            for off in range(0, width, step):
                cols = slice(j0 + off, j0 + off + step)
                for t in range(PACK):
                    nc.tensor.matmul_mx(
                        out=out_banks[t // per_bank][:, t % per_bank, off : off + step],
                        lhsT=wf_codes[:, t * P : (t + 1) * P].bitcast(FP8X4),
                        lhsT_scale=wf_scales[:, t * P : (t + 1) * P],
                        rhs=h_codes[:, cols].bitcast(FP8X4), rhs_scale=h_scales[:, cols],
                        start=True, stop=True,
                    )
            for n, bank in enumerate(out_banks):
                for u in range(per_bank):
                    t = per_bank * n + u
                    nc.scalar.activation(
                        y[:, t * width : (t + 1) * width], bank[:, u, :], IDENTITY, bias=bias[:, t : t + 1]
                    )
                rows = slice(per_bank * n, per_bank * (n + 1))
                nc.sync.dma_start(y_rows[:, rows, j0 : j0 + width], y[:].rearrange("p (t j) -> p t j", t=PACK)[:, rows])
            for j in range(j0, j0 + width, BLOCK):
                scores[j] = y[:].rearrange("p (t j) -> p t j", t=PACK)[:, :, j - j0 :]

        def weave(copy, j0, width):
            copy(
                part(y_bf, j0, width).rearrange("p (c i t) -> p c t i", t=PACK, i=4),
                scores[j0][:, :, 0:width].rearrange("p t (c i) -> p c t i", i=4),
            )

        def planes(j0, width):
            half, off = divmod(j0, HALF)
            nc.vector.quantize_mx(
                out=y_codes[half][:, off : off + width].bitcast(FP8X4), scales=y_scales[:, j0 : j0 + width],
                in_=part(y_bf, j0, width),
            )
            nc.sync.dma_start(y_words[:, j0 : j0 + width], y_codes[half][:, off : off + width].bitcast(I32))

        bounds(0, HALF)
        clip(0)
        clip(256)
        median(0, 256)
        nc.vector.quantize_mx(out=wf_codes[:].bitcast(FP8X4), scales=wf_scales[:], in_=wf_bf[:])
        median(256, 256)
        quantise_h(0, 256)
        quantise_h(256, 256)
        score(0, HALF, (0, 1, 4, 5), HALF)
        bounds(512, 256)
        clip(512)
        pick(highs, sums[A], sums[C], MAX, 768, 256)
        median(512, 256)
        pick(lows, sums[A], sums[C], MIN, 768, 256)
        quantise_h(512, 256)
        score(512, 256, (2, 3), 256)
        clip(768)
        median(768, 128)
        median(896, 128)
        quantise_h(768, 128)
        quantise_h(896, 128)
        score(768, 256, (6, 7), 128)
        weave(nc.vector.tensor_copy, 0, HALF)
        weave(nc.vector.tensor_copy, 512, 256)
        planes(0, HALF)
        planes(512, 256)
        weave(nc.vector.tensor_copy, 768, 128)
        weave(nc.scalar.copy, 896, 128)
        planes(768, 256)
        for q in range(QUADS):
            eng = nc.scalar if q % 2 else nc.sync
            eng.dma_start(out_2[0, 4 * q : 4 * q + 4, :].bitcast(I32), y_scales[32 * q : 32 * q + 4, :].bitcast(I32))
